import numpy as np
import ml_dtypes


def mxq(x, axis, fmt="e4m3"):
    dtype, down = {"e4m3": (ml_dtypes.float8_e4m3fn, 7), "e5m2": (ml_dtypes.float8_e5m2, 14)}[fmt]
    v = np.moveaxis(np.asarray(x, np.float32).astype(ml_dtypes.bfloat16).astype(np.float64), axis, -1)
    blocks = v.reshape(v.shape[:-1] + (-1, 32))
    amax = np.abs(blocks).max(-1, keepdims=True)
    byte = np.maximum(np.where(amax > 0, np.frexp(amax)[1] - 1 + 127, 0) - down, 1)
    scale = np.exp2(byte - 127.0)
    codes = (blocks / scale).astype(np.float32).astype(dtype).astype(np.float64)
    return np.moveaxis((codes * scale).reshape(v.shape), -1, axis)


WIDE = False


def mx_kscale(k):
    if not WIDE:
        return np.ones(k)
    levels = np.array([10, -10, 5, -5, 0])
    if k % 512:
        return np.exp2(np.random.permutation(np.resize(levels, k // 32))).repeat(32)
    a = np.empty((k // 512, 16))
    for p in range(k // 512):
        a[p, :8] = np.random.permutation(np.resize(levels, 8))
        for g in range(8):
            far = levels[np.abs(levels - a[p, g]) >= 10]
            a[p, g + 8] = far[np.random.randint(len(far))]
    return np.exp2(a.ravel()).repeat(32)


def f64(x):
    return np.asarray(x).astype(np.float64)


def striped(idx):
    return np.tile(idx.reshape(-1, 16).T, (8, 1)).astype(np.uint16)


def unstriped(offs):
    return offs[:16].T.reshape(-1).astype(np.int64)


E2M1 = np.array([0.0, 0.5, 1.0, 1.5, 2.0, 3.0, 4.0, 6.0, -0.0, -0.5, -1.0, -1.5, -2.0, -3.0, -4.0, -6.0])


def pack_weight(w, fmt):
    k, n = w.shape
    w = f64(np.asarray(w, np.float32).astype(ml_dtypes.bfloat16)).reshape(k // 32, 32, n)
    amax = np.abs(w).max(1)
    if fmt == "e4m3":
        byte = np.frexp(amax)[1] - 1 + 127 - 7
    else:
        mant, ex = np.frexp(amax / 6.0)
        byte = np.where(mant > 0.5, ex, ex - 1) + 127
    byte = np.clip(np.where(amax > 0, byte, 1), 1, 254)
    scaled = (w * np.exp2(127.0 - byte)[:, None, :]).reshape(k, n).astype(np.float32)
    by_word = np.ascontiguousarray(scaled.reshape(k // 512, 128, 4, n).transpose(0, 1, 3, 2))
    if fmt == "e4m3":
        words = by_word.astype(ml_dtypes.float8_e4m3fn).view(np.uint8)
    else:
        c = by_word.astype(ml_dtypes.float4_e2m1fn).view(np.uint8) & 0xF
        words = (c[..., 0::2] | (c[..., 1::2] << 4)).reshape(k // 512, 128, 2 * n)
    return np.ascontiguousarray(words), np.ascontiguousarray(byte.astype(np.uint8).reshape(k // 512, 16, n))


def unpack_weight(words, scales, fmt):
    g, _, n = scales.shape
    words = np.ascontiguousarray(words).reshape(g, 128, n, -1)
    if fmt == "e4m3":
        vals = words.view(ml_dtypes.float8_e4m3fn).astype(np.float64)
    else:
        nib = np.empty((g, 128, n, 4), np.uint8)
        nib[..., 0::2] = words & 0xF
        nib[..., 1::2] = words >> 4
        vals = E2M1[nib]
    vals = vals * np.repeat(np.exp2(scales.astype(np.float64) - 127.0), 8, axis=1)[..., None]
    return vals.transpose(0, 1, 3, 2).reshape(g * 512, n)


def gelu(v):
    return 0.5 * v * (1.0 + np.tanh(np.sqrt(2.0 / np.pi) * (v + 0.044715 * v**3)))


def pack_table4(v):
    words, scales = pack_weight(v, "e2m1")
    g, t = words.shape[0] // 2, v.shape[1]
    words = words.reshape(g, 2, 128, t, 2).transpose(0, 2, 3, 1, 4)
    return np.concatenate([words.reshape(g, -1), scales.reshape(g, -1)], axis=1)


def unpack_table4(tab):
    g, t = tab.shape[0], tab.shape[1] // 544
    words = tab[:, :512 * t].reshape(g, 128, t, 2, 2).transpose(0, 3, 1, 2, 4).reshape(2 * g, 128, 2 * t)
    return unpack_weight(words, tab[:, 512 * t:].reshape(2 * g, 16, t), "e2m1")


K, T, S, H, N = 2048, 2048, 1024, 1024, 512

def setup_inputs():
    n = np.random.standard_normal
    s = mx_kscale(K)[:, None]
    u = mx_kscale(H)[:, None]
    tab = pack_table4(n((K, T)) * s)
    offs = striped(np.random.permutation(T)[:S])
    wq = (1.5 * n((K, H)) / np.sqrt(K) / s).astype(np.float32)
    gain = (np.exp(0.3 * n((H, 1))) * u)[:, 0].astype(np.float32)
    wmix_words, wmix_scales = pack_weight(2.0 * n((H, N)) / np.sqrt(H) / u, "e2m1")
    bias = (0.5 * n(N)).astype(np.float32)
    return {"tab": tab, "offs": offs, "wq": wq, "gain": gain,
            "wmix_words": wmix_words, "wmix_scales": wmix_scales, "bias": bias}

def reference(tab, offs, wq, gain, wmix_words, wmix_scales, bias):
    v = unpack_table4(tab)[:, unstriped(offs)]
    a = mxq(f64(wq), 0, "e4m3").T @ v
    r = a / (1.0 + np.abs(a))
    h = f64(gain)[:, None] * r
    wmix = unpack_weight(wmix_words, wmix_scales, "e2m1")
    y = wmix.T @ mxq(h, 0, "e4m3")
    return y + f64(bias)[:, None]

@@ -1,0 +1,271 @@
+from contextlib import ExitStack
+
+import concourse.mybir as mybir
+
+K, T, S, H, N = 2048, 2048, 1024, 1024, 512
+FLOPS = 2 * K * H * S + 2 * H * N * S
+
+F32 = mybir.dt.float32
+BF16 = mybir.dt.bfloat16
+I32 = mybir.dt.int32
+U32 = mybir.dt.uint32
+U16 = mybir.dt.uint16
+U8 = mybir.dt.uint8
+FP8X4 = mybir.dt.float8_e4m3fn_x4
+FP4X4 = mybir.dt.float4_e2m1fn_x4
+ACT = mybir.ActivationFunctionType
+ALU = mybir.AluOpType
+
+P = 128
+PACK = 4
+PASS = P * PACK
+K_PASSES = K // PASS
+R_PASSES = H // PASS
+HALF = 512
+HALVES = S // HALF
+LIVE_ROWS = 100
+RAW_BUFS = 3
+SH = (0, 0, 48, 48)
+
+
+def tile_list_shortlist_relevance_mix_kernel(tc, tab, offs, wq, gain, wmix_words, wmix_scales, bias, out):
+    nc = tc.nc
+    with ExitStack() as ctx:
+        keep = ctx.enter_context(tc.tile_pool(name="keep", bufs=1))
+        work = ctx.enter_context(tc.tile_pool(name="work", bufs=2))
+        psum = ctx.enter_context(tc.psum_pool(name="psum", bufs=1))
+
+        offsets = keep.tile([P, S // 16], U16, name="offsets")
+        nc.sync.dma_start(offsets[:], offs)
+
+        tab_scales = work.tile([P, T], U8, name="tab_scales", bufs=1, align_bytes=64)
+        nc.gpsimd.memset(tab_scales[:].bitcast(I32), 0)
+
+        def load_words(m):
+            words = keep.tile([P, T], I32, name="tab_words%d" % m, align_bytes=64)
+            nc.sync.dma_start(words[:], tab[m, : 512 * T].rearrange("(p x) -> p x", p=P).bitcast(I32))
+            return words
+
+        def load_scales(m, r):
+            rows = tab[m, 512 * T :].rearrange("(h quad r x) -> r quad h x", h=2, quad=4, r=4)
+            nc.sync.dma_start(tab_scales[:].bitcast(I32)[4 * m + r : P : 16, :], rows[r].bitcast(I32))
+
+        tab_words = [load_words(0)]
+        for quad in range(3):
+            for m in range(2):
+                load_scales(m, quad)
+
+        one = keep.tile([P, 1], F32, name="one")
+        nc.vector.memset(one[:], 1.0)
+        warm = keep.tile([P, 1], F32, name="warm")
+        nc.scalar.activation(warm[:], one[:], ACT.Abs_reciprocal_sqrt)
+
+        raw = {}
+
+        def load_queries(b, a):
+            raw[b, a] = work.tile([P, PACK, PASS], F32, name="raw", bufs=RAW_BUFS, align_bytes=64)
+            rows = wq[a * PASS : (a + 1) * PASS, b * PASS : (b + 1) * PASS]
+            nc.sync.dma_start(raw[b, a][:], rows.rearrange("(p j) w -> p j w", j=PACK))
+
+        load_queries(0, 0)
+        for m in range(2):
+            load_scales(m, 3)
+        tab_words.append(load_words(1))
+        gains = keep.tile([P, R_PASSES, PACK], F32, name="gains")
+        nc.sync.dma_start(gains[:], gain.rearrange("(b p t) -> p b t", b=R_PASSES, t=PACK))
+
+        def load_mix():
+            mix_words = work.tile([P, R_PASSES, 2 * N], U8, name="mix_words", tag="raw", bufs=RAW_BUFS, align_bytes=64)
+            nc.sync.dma_start(mix_words[:].bitcast(I32), wmix_words.rearrange("b p x -> p b x").bitcast(I32))
+            mix_scales = work.tile([P, R_PASSES, N], U8, name="mix_scales", tag="raw", bufs=RAW_BUFS, align_bytes=64)
+            nc.gpsimd.memset(mix_scales[:].bitcast(I32), 0)
+            for quad in range(4):
+                nc.sync.dma_start(
+                    mix_scales[:].bitcast(I32)[32 * quad : 32 * quad + 4, :, :],
+                    wmix_scales[:, 4 * quad : 4 * quad + 4, :].rearrange("b r x -> r b x").bitcast(I32),
+                )
+            biases = work.tile([P, N // P], F32, name="biases", tag="raw", bufs=RAW_BUFS, align_bytes=64)
+            with nc.allow_non_contiguous_dma(reason="one bias value a partition"):
+                nc.sync.dma_start(biases[:], bias.rearrange("(c p) -> p c", p=P))
+            return mix_words, mix_scales, biases
+
+        v_scales = [keep.tile([P, S], U8, name="v_scales%d" % a, align_bytes=64) for a in range(K_PASSES)]
+        for a in range(1, K_PASSES):
+            nc.vector.memset(v_scales[a][:].bitcast(I32), 0)
+
+        v_words = {}
+
+        def gather_words(m, half, tag, bufs):
+            picked = work.tile([P, HALF], U32, name="picked", tag=tag, bufs=bufs, align_bytes=64)
+            cols = slice(half * HALF // 16, (half + 1) * HALF // 16)
+            nc.vector.tensor_copy(picked[:], tab_words[m][:].bitcast(U32).indirect(offsets[:, cols]))
+            parted = keep.tile([P, 2, 2 * HALF], U8, name="parted%d%d" % (m, half), align_bytes=64)
+            nc.vector.tensor_copy(parted[:].bitcast(U16), picked[:].bitcast(U16).rearrange("p (j h) -> p h j", h=2))
+            for h in range(2):
+                v_words[2 * m + h, half] = parted[:, h, :]
+
+        def gather_scales():
+            nc.vector.tensor_copy(v_scales[0][:], tab_scales[:].indirect(offsets[:]))
+            for a in range(1, K_PASSES):
+                first = 16 * (a % 2) + 4 * (a // 2)
+                nc.gpsimd.dma_start(
+                    v_scales[a][:].bitcast(I32)[0:LIVE_ROWS, :],
+                    v_scales[0][:].bitcast(I32)[first : first + LIVE_ROWS, :],
+                )
+
+        q_codes, q_scales = {}, {}
+
+        def quantize_queries(b, a, scalar_share, tag="grouped", bufs=3):
+            grouped = work.tile([P, PACK * PASS], BF16, name="grouped", tag=tag, bufs=bufs, align_bytes=64)
+            if (b, a) not in raw:
+                load_queries(b, a)
+            src = raw[b, a][:].rearrange("p j (m t) -> p m j t", t=PACK)
+            dst = grouped[:].rearrange("p (t m j) -> p m j t", t=PACK, j=PACK)
+            if scalar_share > 0:
+                nc.scalar.copy(dst[:, :scalar_share], src[:, :scalar_share])
+            if scalar_share < P:
+                nc.vector.tensor_copy(dst[:, scalar_share:], src[:, scalar_share:])
+            q_codes[b, a] = keep.tile([P, PASS], U32, name="q_codes%d%d" % (b, a), align_bytes=64)
+            q_scales[b, a] = keep.tile([P, PASS], U8, name="q_scales%d%d" % (b, a), align_bytes=64)
+            nc.vector.quantize_mx(q_codes[b, a][:].bitcast(FP8X4), q_scales[b, a][:], grouped[:])
+
+        h_codes, h_scales = {}, {}
+
+        def products(b, half):
+            banks = [psum.tile([P, HALF], F32, name="acc", tag="bank%d" % (PACK * half + t)) for t in range(PACK)]
+            if (b, half) == (0, 1):
+                order = [(0, t) for t in range(PACK)] + [(a, t) for t in range(PACK) for a in (2, 3, 1)]
+            else:
+                order = [(a, t) for a in range(K_PASSES) for t in range(PACK)]
+            last = {t: a for a, t in order}
+            for a, t in order:
+                if True:
+                    cols = slice(t * P, (t + 1) * P)
+                    nc.tensor.matmul_mx(
+                        banks[t][:],
+                        lhsT=q_codes[b, a][:, cols].bitcast(FP8X4),
+                        lhsT_scale=q_scales[b, a][:, cols],
+                        rhs=v_words[a, half].bitcast(FP4X4),
+                        rhs_scale=v_scales[a][:, half * HALF : (half + 1) * HALF],
+                        start=(a == 0),
+                        stop=(a == last[t]),
+                    )
+            return banks
+
+        def relevance(b, half, banks):
+            root = work.tile([P, PACK, HALF], F32, name="root", bufs=3, align_bytes=64)
+            partial = work.tile([P, PACK, HALF], F32, name="partial", bufs=3, align_bytes=64)
+            for t in range(PACK):
+                size = work.tile([P, HALF], F32, name="size", bufs=3, align_bytes=64)
+                nc.scalar.activation(size[:], banks[t][:], ACT.Abs)
+                nc.scalar.activation(root[:, t, :], size[:], ACT.Abs_reciprocal_sqrt, bias=one[:])
+                nc.vector.scalar_tensor_tensor(
+                    partial[:, t, :], banks[t][:], gains[:, b, t : t + 1], root[:, t, :], ALU.mult, ALU.mult
+                )
+            return root, partial
+
+        def quantize_relevance(b, half, root, partial):
+            rounded = work.tile([P, PACK * HALF], BF16, name="rounded", align_bytes=64)
+            nc.vector.tensor_tensor(
+                rounded[:].rearrange("p (c i t) -> p c t i", i=4, t=PACK),
+                partial[:].rearrange("p t (c i) -> p c t i", i=4),
+                root[:].rearrange("p t (c i) -> p c t i", i=4),
+                ALU.mult,
+            )
+            h_codes[b, half] = keep.tile([P, HALF], U32, name="h_codes%d%d" % (b, half), align_bytes=64)
+            h_scales[b, half] = keep.tile([P, HALF], U8, name="h_scales%d%d" % (b, half), align_bytes=64)
+            nc.vector.quantize_mx(h_codes[b, half][:].bitcast(FP8X4), h_scales[b, half][:], rounded[:])
+
+        def mix(half):
+            for c in range(N // P):
+                bank = psum.tile([P, HALF], F32, name="score", tag="bank%d" % (PACK * half + c))
+                for b in range(R_PASSES):
+                    nc.tensor.matmul_mx(
+                        bank[:],
+                        lhsT=mix_words[:, b, 2 * c * P : 2 * (c + 1) * P].bitcast(FP4X4),
+                        lhsT_scale=mix_scales[:, b, c * P : (c + 1) * P],
+                        rhs=h_codes[b, half][:].bitcast(FP8X4),
+                        rhs_scale=h_scales[b, half][:],
+                        start=(b == 0),
+                        stop=(b == R_PASSES - 1),
+                    )
+                result = work.tile([P, HALF], F32, name="result", bufs=8, align_bytes=64)
+                nc.scalar.activation(result[:], bank[:], ACT.Identity, bias=biases[:, c : c + 1])
+                nc.sync.dma_start(out[c * P : (c + 1) * P, half * HALF : (half + 1) * HALF], result[:])
+
+        def last_relevance(b, banks):
+            flat = keep.tile([P, PACK, HALF], BF16, name="flat", align_bytes=64)
+            for t in range(PACK):
+                size = work.tile([P, HALF], F32, name="size", bufs=3, align_bytes=64)
+                nc.scalar.activation(size[:], banks[t][:], ACT.Abs)
+                root = work.tile([P, HALF], F32, name="root_last", bufs=3, align_bytes=64)
+                nc.scalar.activation(root[:], size[:], ACT.Abs_reciprocal_sqrt, bias=one[:])
+                inverse = work.tile([P, HALF], F32, name="inverse", bufs=4, align_bytes=64)
+                nc.scalar.activation(inverse[:], root[:], ACT.Square)
+                nc.vector.scalar_tensor_tensor(
+                    flat[:, t, :], banks[t][:], gains[:, b, t : t + 1], inverse[:], ALU.mult, ALU.mult
+                )
+            return flat
+
+        def finish_in_pieces(half, flat):
+            for piece in range(HALF // P):
+                cols = slice(piece * P, (piece + 1) * P)
+                rounded = work.tile([P, PACK * P], BF16, name="rounded_piece", bufs=4, align_bytes=64)
+                nc.vector.tensor_copy(
+                    rounded[:].rearrange("p (c i t) -> p c t i", i=4, t=PACK),
+                    flat[:, :, cols].rearrange("p t (c i) -> p c t i", i=4),
+                )
+                codes = work.tile([P, P], U32, name="codes_piece", bufs=4, align_bytes=64)
+                scales = work.tile([P, P], U8, name="scales_piece", bufs=4, align_bytes=64)
+                nc.vector.quantize_mx(codes[:].bitcast(FP8X4), scales[:], rounded[:])
+                operands = [(h_codes[0, half][:, cols], h_scales[0, half][:, cols]), (codes[:], scales[:])]
+                bank = psum.tile([P, N // P, P], F32, name="score_piece", tag="bank%d" % (PACK * half + piece))
+                result = work.tile([P, N // P, P], F32, name="result_piece", bufs=4, align_bytes=64)
+                for b in range(R_PASSES):
+                    for c in range(N // P):
+                        nc.tensor.matmul_mx(
+                            bank[:, c, :],
+                            lhsT=mix_words[:, b, 2 * c * P : 2 * (c + 1) * P].bitcast(FP4X4),
+                            lhsT_scale=mix_scales[:, b, c * P : (c + 1) * P],
+                            rhs=operands[b][0].bitcast(FP8X4),
+                            rhs_scale=operands[b][1],
+                            start=(b == 0 and c == 0),
+                            stop=(b == R_PASSES - 1 and c == N // P - 1),
+                        )
+                if piece < HALF // P - 1:
+                    for c in range(N // P):
+                        nc.scalar.activation(result[:, c, :], bank[:, c, :], ACT.Identity, bias=biases[:, c : c + 1])
+                else:
+                    nc.vector.tensor_tensor(
+                        result[:], bank[:], biases[:].unsqueeze(2).to_broadcast([P, N // P, P]), ALU.add
+                    )
+                first = half * HALF + piece * P
+                nc.sync.dma_start(out[:, first : first + P].rearrange("(c p) j -> p c j", p=P), result[:])
+
+        gather_words(0, 0, "picked", 1)
+        gather_scales()
+        quantize_queries(0, 0, P, "first", 1)
+        gather_words(1, 0, "picked", 1)
+        gather_words(0, 1, "first", 1)
+        quantize_queries(0, 1, P)
+        quantize_queries(0, 2, 48)
+        quantize_queries(0, 3, 48, "last", 1)
+        banks00 = products(0, 0)
+        gather_words(1, 1, "last", 1)
+        banks01 = products(0, 1)
+        quantize_queries(1, 0, SH[0])
+        quantize_queries(1, 1, SH[1])
+        quantize_queries(1, 2, SH[2])
+        quantize_queries(1, 3, SH[3])
+        parts00 = relevance(0, 0, banks00)
+        parts01 = relevance(0, 1, banks01)
+        mix_words, mix_scales, biases = load_mix()
+        banks10 = products(1, 0)
+        banks11 = products(1, 1)
+        parts10 = relevance(1, 0, banks10)
+        quantize_relevance(0, 0, *parts00)
+        quantize_relevance(1, 0, *parts10)
+        flat = last_relevance(1, banks11)
+        quantize_relevance(0, 1, *parts01)
+        mix(0)
+        finish_in_pieces(1, flat)

@@ -22,10 +22,11 @@ PASS = P * PACK
 K_PASSES = K // PASS
 R_PASSES = H // PASS
 HALF = 512
-HALVES = S // HALF
+WORD_BYTES = 512 * T
 LIVE_ROWS = 100
-RAW_BUFS = 3
-SH = (0, 0, 48, 48)
+SPREAD_ROWS = 112
+STAGES = 3
+SCALAR_SHARE = 48
 
 
 def tile_list_shortlist_relevance_mix_kernel(tc, tab, offs, wq, gain, wmix_words, wmix_scales, bias, out):
@@ -41,53 +42,52 @@ def tile_list_shortlist_relevance_mix_kernel(tc, tab, offs, wq, gain, wmix_words
         tab_scales = work.tile([P, T], U8, name="tab_scales", bufs=1, align_bytes=64)
         nc.gpsimd.memset(tab_scales[:].bitcast(I32), 0)
 
-        def load_words(m):
+        def load_table_words(m):
             words = keep.tile([P, T], I32, name="tab_words%d" % m, align_bytes=64)
-            nc.sync.dma_start(words[:], tab[m, : 512 * T].rearrange("(p x) -> p x", p=P).bitcast(I32))
+            nc.sync.dma_start(words[:], tab[m, :WORD_BYTES].rearrange("(p x) -> p x", p=P).bitcast(I32))
             return words
 
-        def load_scales(m, r):
-            rows = tab[m, 512 * T :].rearrange("(h quad r x) -> r quad h x", h=2, quad=4, r=4)
-            nc.sync.dma_start(tab_scales[:].bitcast(I32)[4 * m + r : P : 16, :], rows[r].bitcast(I32))
-
-        tab_words = [load_words(0)]
-        for quad in range(3):
+        def load_table_scales(r):
             for m in range(2):
-                load_scales(m, quad)
+                rows = tab[m, WORD_BYTES:].rearrange("(h quad r x) -> r quad h x", h=2, quad=4, r=4)
+                nc.sync.dma_start(tab_scales[:].bitcast(I32)[4 * m + r : P : 16, :], rows[r].bitcast(I32))
+
+        staged = {}
+
+        def load_queries(b, a):
+            staged[b, a] = work.tile([P, PACK, PASS], F32, name="raw", bufs=STAGES, align_bytes=64)
+            rows = wq[a * PASS : (a + 1) * PASS, b * PASS : (b + 1) * PASS]
+            nc.sync.dma_start(staged[b, a][:], rows.rearrange("(p i) c -> p i c", i=PACK))
+
+        tab_words = [load_table_words(0)]
+        for r in range(3):
+            load_table_scales(r)
 
         one = keep.tile([P, 1], F32, name="one")
         nc.vector.memset(one[:], 1.0)
         warm = keep.tile([P, 1], F32, name="warm")
         nc.scalar.activation(warm[:], one[:], ACT.Abs_reciprocal_sqrt)
 
-        raw = {}
-
-        def load_queries(b, a):
-            raw[b, a] = work.tile([P, PACK, PASS], F32, name="raw", bufs=RAW_BUFS, align_bytes=64)
-            rows = wq[a * PASS : (a + 1) * PASS, b * PASS : (b + 1) * PASS]
-            nc.sync.dma_start(raw[b, a][:], rows.rearrange("(p j) w -> p j w", j=PACK))
-
         load_queries(0, 0)
-        for m in range(2):
-            load_scales(m, 3)
-        tab_words.append(load_words(1))
+        load_table_scales(3)
+        tab_words.append(load_table_words(1))
         gains = keep.tile([P, R_PASSES, PACK], F32, name="gains")
         nc.sync.dma_start(gains[:], gain.rearrange("(b p t) -> p b t", b=R_PASSES, t=PACK))
 
         def load_mix():
-            mix_words = work.tile([P, R_PASSES, 2 * N], U8, name="mix_words", tag="raw", bufs=RAW_BUFS, align_bytes=64)
-            nc.sync.dma_start(mix_words[:].bitcast(I32), wmix_words.rearrange("b p x -> p b x").bitcast(I32))
-            mix_scales = work.tile([P, R_PASSES, N], U8, name="mix_scales", tag="raw", bufs=RAW_BUFS, align_bytes=64)
-            nc.gpsimd.memset(mix_scales[:].bitcast(I32), 0)
+            words = work.tile([P, R_PASSES, 2 * N], U8, name="mix_words", tag="raw", bufs=STAGES, align_bytes=64)
+            nc.sync.dma_start(words[:].bitcast(I32), wmix_words.rearrange("b p x -> p b x").bitcast(I32))
+            scales = work.tile([P, R_PASSES, N], U8, name="mix_scales", tag="raw", bufs=STAGES, align_bytes=64)
+            nc.gpsimd.memset(scales[:].bitcast(I32), 0)
             for quad in range(4):
                 nc.sync.dma_start(
-                    mix_scales[:].bitcast(I32)[32 * quad : 32 * quad + 4, :, :],
+                    scales[:].bitcast(I32)[32 * quad : 32 * quad + 4, :, :],
                     wmix_scales[:, 4 * quad : 4 * quad + 4, :].rearrange("b r x -> r b x").bitcast(I32),
                 )
-            biases = work.tile([P, N // P], F32, name="biases", tag="raw", bufs=RAW_BUFS, align_bytes=64)
-            with nc.allow_non_contiguous_dma(reason="one bias value a partition"):
-                nc.sync.dma_start(biases[:], bias.rearrange("(c p) -> p c", p=P))
-            return mix_words, mix_scales, biases
+            columns = work.tile([P, N // P], F32, name="biases", tag="raw", bufs=STAGES, align_bytes=64)
+            with nc.allow_non_contiguous_dma(reason="one bias value for each partition and output tile"):
+                nc.sync.dma_start(columns[:], bias.rearrange("(c p) -> p c", p=P))
+            return words, scales, columns
 
         v_scales = [keep.tile([P, S], U8, name="v_scales%d" % a, align_bytes=64) for a in range(K_PASSES)]
         for a in range(1, K_PASSES):
@@ -95,10 +95,10 @@ def tile_list_shortlist_relevance_mix_kernel(tc, tab, offs, wq, gain, wmix_words
 
         v_words = {}
 
-        def gather_words(m, half, tag, bufs):
-            picked = work.tile([P, HALF], U32, name="picked", tag=tag, bufs=bufs, align_bytes=64)
-            cols = slice(half * HALF // 16, (half + 1) * HALF // 16)
-            nc.vector.tensor_copy(picked[:], tab_words[m][:].bitcast(U32).indirect(offsets[:, cols]))
+        def gather_words(m, half, tag):
+            picked = work.tile([P, HALF], U32, name="picked", tag=tag, bufs=1, align_bytes=64)
+            entries = slice(half * HALF // 16, (half + 1) * HALF // 16)
+            nc.vector.tensor_copy(picked[:], tab_words[m][:].bitcast(U32).indirect(offsets[:, entries]))
             parted = keep.tile([P, 2, 2 * HALF], U8, name="parted%d%d" % (m, half), align_bytes=64)
             nc.vector.tensor_copy(parted[:].bitcast(U16), picked[:].bitcast(U16).rearrange("p (j h) -> p h j", h=2))
             for h in range(2):
@@ -107,52 +107,50 @@ def tile_list_shortlist_relevance_mix_kernel(tc, tab, offs, wq, gain, wmix_words
         def gather_scales():
             nc.vector.tensor_copy(v_scales[0][:], tab_scales[:].indirect(offsets[:]))
             for a in range(1, K_PASSES):
-                first = 16 * (a % 2) + 4 * (a // 2)
-                nc.gpsimd.dma_start(
-                    v_scales[a][:].bitcast(I32)[0:LIVE_ROWS, :],
-                    v_scales[0][:].bitcast(I32)[first : first + LIVE_ROWS, :],
-                )
+                lower = 16 * (a % 2) + 4 * (a // 2)
+                runs = [(0, SPREAD_ROWS)] if lower + SPREAD_ROWS <= P else [(0, 96), (96, LIVE_ROWS)]
+                for begin, end in runs:
+                    nc.scalar.dma_start(
+                        v_scales[a][:].bitcast(I32)[begin:end, :],
+                        v_scales[0][:].bitcast(I32)[lower + begin : lower + end, :],
+                    )
 
         q_codes, q_scales = {}, {}
 
         def quantize_queries(b, a, scalar_share, tag="grouped", bufs=3):
             grouped = work.tile([P, PACK * PASS], BF16, name="grouped", tag=tag, bufs=bufs, align_bytes=64)
-            if (b, a) not in raw:
+            if (b, a) not in staged:
                 load_queries(b, a)
-            src = raw[b, a][:].rearrange("p j (m t) -> p m j t", t=PACK)
-            dst = grouped[:].rearrange("p (t m j) -> p m j t", t=PACK, j=PACK)
+            src = staged[b, a][:].rearrange("p i (u t) -> p u i t", t=PACK)
+            dst = grouped[:].rearrange("p (t u i) -> p u i t", t=PACK, i=PACK)
+            q_codes[b, a] = keep.tile([P, PASS], U32, name="q_codes%d%d" % (b, a), align_bytes=64)
+            q_scales[b, a] = keep.tile([P, PASS], U8, name="q_scales%d%d" % (b, a), align_bytes=64)
             if scalar_share > 0:
                 nc.scalar.copy(dst[:, :scalar_share], src[:, :scalar_share])
             if scalar_share < P:
                 nc.vector.tensor_copy(dst[:, scalar_share:], src[:, scalar_share:])
-            q_codes[b, a] = keep.tile([P, PASS], U32, name="q_codes%d%d" % (b, a), align_bytes=64)
-            q_scales[b, a] = keep.tile([P, PASS], U8, name="q_scales%d%d" % (b, a), align_bytes=64)
             nc.vector.quantize_mx(q_codes[b, a][:].bitcast(FP8X4), q_scales[b, a][:], grouped[:])
 
-        h_codes, h_scales = {}, {}
-
-        def products(b, half):
+        def products(b, half, order):
             banks = [psum.tile([P, HALF], F32, name="acc", tag="bank%d" % (PACK * half + t)) for t in range(PACK)]
-            if (b, half) == (0, 1):
-                order = [(0, t) for t in range(PACK)] + [(a, t) for t in range(PACK) for a in (2, 3, 1)]
-            else:
-                order = [(a, t) for a in range(K_PASSES) for t in range(PACK)]
             last = {t: a for a, t in order}
             for a, t in order:
-                if True:
-                    cols = slice(t * P, (t + 1) * P)
-                    nc.tensor.matmul_mx(
-                        banks[t][:],
-                        lhsT=q_codes[b, a][:, cols].bitcast(FP8X4),
-                        lhsT_scale=q_scales[b, a][:, cols],
-                        rhs=v_words[a, half].bitcast(FP4X4),
-                        rhs_scale=v_scales[a][:, half * HALF : (half + 1) * HALF],
-                        start=(a == 0),
-                        stop=(a == last[t]),
-                    )
+                cols = slice(t * P, (t + 1) * P)
+                nc.tensor.matmul_mx(
+                    banks[t][:],
+                    lhsT=q_codes[b, a][:, cols].bitcast(FP8X4),
+                    lhsT_scale=q_scales[b, a][:, cols],
+                    rhs=v_words[a, half].bitcast(FP4X4),
+                    rhs_scale=v_scales[a][:, half * HALF : (half + 1) * HALF],
+                    start=(a == 0),
+                    stop=(a == last[t]),
+                )
             return banks
 
-        def relevance(b, half, banks):
+        pass_by_pass = [(a, t) for a in range(K_PASSES) for t in range(PACK)]
+        bank_by_bank = [(0, t) for t in range(PACK)] + [(a, t) for t in range(PACK) for a in (2, 3, 1)]
+
+        def relevance(b, banks):
             root = work.tile([P, PACK, HALF], F32, name="root", bufs=3, align_bytes=64)
             partial = work.tile([P, PACK, HALF], F32, name="partial", bufs=3, align_bytes=64)
             for t in range(PACK):
@@ -164,17 +162,33 @@ def tile_list_shortlist_relevance_mix_kernel(tc, tab, offs, wq, gain, wmix_words
                 )
             return root, partial
 
+        h_codes, h_scales = {}, {}
+
         def quantize_relevance(b, half, root, partial):
             rounded = work.tile([P, PACK * HALF], BF16, name="rounded", align_bytes=64)
             nc.vector.tensor_tensor(
-                rounded[:].rearrange("p (c i t) -> p c t i", i=4, t=PACK),
-                partial[:].rearrange("p t (c i) -> p c t i", i=4),
-                root[:].rearrange("p t (c i) -> p c t i", i=4),
+                rounded[:].rearrange("p (g e t) -> p g t e", e=4, t=PACK),
+                partial[:].rearrange("p t (g e) -> p g t e", e=4),
+                root[:].rearrange("p t (g e) -> p g t e", e=4),
                 ALU.mult,
             )
             h_codes[b, half] = keep.tile([P, HALF], U32, name="h_codes%d%d" % (b, half), align_bytes=64)
             h_scales[b, half] = keep.tile([P, HALF], U8, name="h_scales%d%d" % (b, half), align_bytes=64)
             nc.vector.quantize_mx(h_codes[b, half][:].bitcast(FP8X4), h_scales[b, half][:], rounded[:])
+
+        def last_relevance(b, banks):
+            flat = keep.tile([P, PACK, HALF], BF16, name="flat", align_bytes=64)
+            for t in range(PACK):
+                size = work.tile([P, HALF], F32, name="size", bufs=3, align_bytes=64)
+                nc.scalar.activation(size[:], banks[t][:], ACT.Abs)
+                root = work.tile([P, HALF], F32, name="root_last", bufs=3, align_bytes=64)
+                nc.scalar.activation(root[:], size[:], ACT.Abs_reciprocal_sqrt, bias=one[:])
+                inverse = work.tile([P, HALF], F32, name="inverse", bufs=PACK, align_bytes=64)
+                nc.scalar.activation(inverse[:], root[:], ACT.Square)
+                nc.vector.scalar_tensor_tensor(
+                    flat[:, t, :], banks[t][:], gains[:, b, t : t + 1], inverse[:], ALU.mult, ALU.mult
+                )
+            return flat
 
         def mix(half):
             for c in range(N // P):
@@ -193,34 +207,21 @@ def tile_list_shortlist_relevance_mix_kernel(tc, tab, offs, wq, gain, wmix_words
                 nc.scalar.activation(result[:], bank[:], ACT.Identity, bias=biases[:, c : c + 1])
                 nc.sync.dma_start(out[c * P : (c + 1) * P, half * HALF : (half + 1) * HALF], result[:])
 
-        def last_relevance(b, banks):
-            flat = keep.tile([P, PACK, HALF], BF16, name="flat", align_bytes=64)
-            for t in range(PACK):
-                size = work.tile([P, HALF], F32, name="size", bufs=3, align_bytes=64)
-                nc.scalar.activation(size[:], banks[t][:], ACT.Abs)
-                root = work.tile([P, HALF], F32, name="root_last", bufs=3, align_bytes=64)
-                nc.scalar.activation(root[:], size[:], ACT.Abs_reciprocal_sqrt, bias=one[:])
-                inverse = work.tile([P, HALF], F32, name="inverse", bufs=4, align_bytes=64)
-                nc.scalar.activation(inverse[:], root[:], ACT.Square)
-                nc.vector.scalar_tensor_tensor(
-                    flat[:, t, :], banks[t][:], gains[:, b, t : t + 1], inverse[:], ALU.mult, ALU.mult
-                )
-            return flat
-
-        def finish_in_pieces(half, flat):
-            for piece in range(HALF // P):
+        def mix_in_pieces(half, flat):
+            pieces = HALF // P
+            for piece in range(pieces):
                 cols = slice(piece * P, (piece + 1) * P)
-                rounded = work.tile([P, PACK * P], BF16, name="rounded_piece", bufs=4, align_bytes=64)
+                rounded = work.tile([P, PACK * P], BF16, name="rounded_piece", bufs=pieces, align_bytes=64)
                 nc.vector.tensor_copy(
-                    rounded[:].rearrange("p (c i t) -> p c t i", i=4, t=PACK),
-                    flat[:, :, cols].rearrange("p t (c i) -> p c t i", i=4),
+                    rounded[:].rearrange("p (g e t) -> p g t e", e=4, t=PACK),
+                    flat[:, :, cols].rearrange("p t (g e) -> p g t e", e=4),
                 )
-                codes = work.tile([P, P], U32, name="codes_piece", bufs=4, align_bytes=64)
-                scales = work.tile([P, P], U8, name="scales_piece", bufs=4, align_bytes=64)
+                codes = work.tile([P, P], U32, name="codes_piece", bufs=pieces, align_bytes=64)
+                scales = work.tile([P, P], U8, name="scales_piece", bufs=pieces, align_bytes=64)
                 nc.vector.quantize_mx(codes[:].bitcast(FP8X4), scales[:], rounded[:])
                 operands = [(h_codes[0, half][:, cols], h_scales[0, half][:, cols]), (codes[:], scales[:])]
                 bank = psum.tile([P, N // P, P], F32, name="score_piece", tag="bank%d" % (PACK * half + piece))
-                result = work.tile([P, N // P, P], F32, name="result_piece", bufs=4, align_bytes=64)
+                result = work.tile([P, N // P, P], F32, name="result_piece", bufs=pieces, align_bytes=64)
                 for b in range(R_PASSES):
                     for c in range(N // P):
                         nc.tensor.matmul_mx(
@@ -232,7 +233,7 @@ def tile_list_shortlist_relevance_mix_kernel(tc, tab, offs, wq, gain, wmix_words
                             start=(b == 0 and c == 0),
                             stop=(b == R_PASSES - 1 and c == N // P - 1),
                         )
-                if piece < HALF // P - 1:
+                if piece < pieces - 1:
                     for c in range(N // P):
                         nc.scalar.activation(result[:, c, :], bank[:, c, :], ACT.Identity, bias=biases[:, c : c + 1])
                 else:
@@ -242,30 +243,28 @@ def tile_list_shortlist_relevance_mix_kernel(tc, tab, offs, wq, gain, wmix_words
                 first = half * HALF + piece * P
                 nc.sync.dma_start(out[:, first : first + P].rearrange("(c p) j -> p c j", p=P), result[:])
 
-        gather_words(0, 0, "picked", 1)
+        gather_words(0, 0, "picked")
         gather_scales()
         quantize_queries(0, 0, P, "first", 1)
-        gather_words(1, 0, "picked", 1)
-        gather_words(0, 1, "first", 1)
+        gather_words(1, 0, "picked")
+        gather_words(0, 1, "first")
         quantize_queries(0, 1, P)
-        quantize_queries(0, 2, 48)
-        quantize_queries(0, 3, 48, "last", 1)
-        banks00 = products(0, 0)
-        gather_words(1, 1, "last", 1)
-        banks01 = products(0, 1)
-        quantize_queries(1, 0, SH[0])
-        quantize_queries(1, 1, SH[1])
-        quantize_queries(1, 2, SH[2])
-        quantize_queries(1, 3, SH[3])
-        parts00 = relevance(0, 0, banks00)
-        parts01 = relevance(0, 1, banks01)
+        quantize_queries(0, 2, SCALAR_SHARE)
+        quantize_queries(0, 3, SCALAR_SHARE, "last", 1)
+        banks00 = products(0, 0, pass_by_pass)
+        gather_words(1, 1, "last")
+        banks01 = products(0, 1, bank_by_bank)
+        for a in range(K_PASSES):
+            quantize_queries(1, a, 0 if a < K_PASSES // 2 else SCALAR_SHARE)
+        parts00 = relevance(0, banks00)
+        parts01 = relevance(0, banks01)
         mix_words, mix_scales, biases = load_mix()
-        banks10 = products(1, 0)
-        banks11 = products(1, 1)
-        parts10 = relevance(1, 0, banks10)
+        banks10 = products(1, 0, pass_by_pass)
+        banks11 = products(1, 1, pass_by_pass)
+        parts10 = relevance(1, banks10)
         quantize_relevance(0, 0, *parts00)
         quantize_relevance(1, 0, *parts10)
-        flat = last_relevance(1, banks11)
+        flat11 = last_relevance(1, banks11)
         quantize_relevance(0, 1, *parts01)
         mix(0)
-        finish_in_pieces(1, flat)
+        mix_in_pieces(1, flat11)

@@ -25,7 +25,7 @@ HALF = 512
 WORD_BYTES = 512 * T
 LIVE_ROWS = 100
 SPREAD_ROWS = 112
-STAGES = 3
+STAGES = 4
 SCALAR_SHARE = 48
 
 
@@ -39,18 +39,16 @@ def tile_list_shortlist_relevance_mix_kernel(tc, tab, offs, wq, gain, wmix_words
         offsets = keep.tile([P, S // 16], U16, name="offsets")
         nc.sync.dma_start(offsets[:], offs)
 
-        tab_scales = work.tile([P, T], U8, name="tab_scales", bufs=1, align_bytes=64)
-        nc.gpsimd.memset(tab_scales[:].bitcast(I32), 0)
+        tab_scales = keep.tile([P, T], U8, name="tab_scales", align_bytes=64)
+        nc.gpsimd.memset(tab_scales[:].bitcast(I32)[P // 2 :, :], 0)
+        for m in range(2):
+            rows = tab[m, WORD_BYTES:].rearrange("(h q x) -> q h x", h=2, q=16)
+            nc.sync.dma_start(tab_scales[:].bitcast(I32)[m : P // 2 : 2, :], rows.bitcast(I32))
 
         def load_table_words(m):
             words = keep.tile([P, T], I32, name="tab_words%d" % m, align_bytes=64)
             nc.sync.dma_start(words[:], tab[m, :WORD_BYTES].rearrange("(p x) -> p x", p=P).bitcast(I32))
             return words
-
-        def load_table_scales(r):
-            for m in range(2):
-                rows = tab[m, WORD_BYTES:].rearrange("(h quad r x) -> r quad h x", h=2, quad=4, r=4)
-                nc.sync.dma_start(tab_scales[:].bitcast(I32)[4 * m + r : P : 16, :], rows[r].bitcast(I32))
 
         staged = {}
 
@@ -60,8 +58,6 @@ def tile_list_shortlist_relevance_mix_kernel(tc, tab, offs, wq, gain, wmix_words
             nc.sync.dma_start(staged[b, a][:], rows.rearrange("(p i) c -> p i c", i=PACK))
 
         tab_words = [load_table_words(0)]
-        for r in range(3):
-            load_table_scales(r)
 
         one = keep.tile([P, 1], F32, name="one")
         nc.vector.memset(one[:], 1.0)
@@ -69,7 +65,6 @@ def tile_list_shortlist_relevance_mix_kernel(tc, tab, offs, wq, gain, wmix_words
         nc.scalar.activation(warm[:], one[:], ACT.Abs_reciprocal_sqrt)
 
         load_queries(0, 0)
-        load_table_scales(3)
         tab_words.append(load_table_words(1))
         gains = keep.tile([P, R_PASSES, PACK], F32, name="gains")
         nc.sync.dma_start(gains[:], gain.rearrange("(b p t) -> p b t", b=R_PASSES, t=PACK))
@@ -89,9 +84,8 @@ def tile_list_shortlist_relevance_mix_kernel(tc, tab, offs, wq, gain, wmix_words
                 nc.sync.dma_start(columns[:], bias.rearrange("(c p) -> p c", p=P))
             return words, scales, columns
 
-        v_scales = [keep.tile([P, S], U8, name="v_scales%d" % a, align_bytes=64) for a in range(K_PASSES)]
-        for a in range(1, K_PASSES):
-            nc.vector.memset(v_scales[a][:].bitcast(I32), 0)
+        v_scales = keep.tile([P, K_PASSES, S], U8, name="v_scales", align_bytes=64)
+        nc.gpsimd.memset(v_scales[:].bitcast(I32), 0)
 
         v_words = {}
 
@@ -105,15 +99,13 @@ def tile_list_shortlist_relevance_mix_kernel(tc, tab, offs, wq, gain, wmix_words
                 v_words[2 * m + h, half] = parted[:, h, :]
 
         def gather_scales():
-            nc.vector.tensor_copy(v_scales[0][:], tab_scales[:].indirect(offsets[:]))
-            for a in range(1, K_PASSES):
-                lower = 16 * (a % 2) + 4 * (a // 2)
-                runs = [(0, SPREAD_ROWS)] if lower + SPREAD_ROWS <= P else [(0, 96), (96, LIVE_ROWS)]
-                for begin, end in runs:
-                    nc.scalar.dma_start(
-                        v_scales[a][:].bitcast(I32)[begin:end, :],
-                        v_scales[0][:].bitcast(I32)[lower + begin : lower + end, :],
-                    )
+            picked = keep.tile([P, S], U8, name="picked_scales", align_bytes=64)
+            nc.vector.tensor_copy(picked[:], tab_scales[:].indirect(offsets[:]))
+            for quad in range(4):
+                nc.scalar.dma_start(
+                    v_scales[:].bitcast(I32)[32 * quad : 32 * quad + 4, :, :],
+                    picked[:].bitcast(I32)[16 * quad : 16 * quad + 16, :],
+                )
 
         q_codes, q_scales = {}, {}
 
@@ -141,7 +133,7 @@ def tile_list_shortlist_relevance_mix_kernel(tc, tab, offs, wq, gain, wmix_words
                     lhsT=q_codes[b, a][:, cols].bitcast(FP8X4),
                     lhsT_scale=q_scales[b, a][:, cols],
                     rhs=v_words[a, half].bitcast(FP4X4),
-                    rhs_scale=v_scales[a][:, half * HALF : (half + 1) * HALF],
+                    rhs_scale=v_scales[:, 2 * (a % 2) + a // 2, half * HALF : (half + 1) * HALF],
                     start=(a == 0),
                     stop=(a == last[t]),
                 )
@@ -243,8 +235,8 @@ def tile_list_shortlist_relevance_mix_kernel(tc, tab, offs, wq, gain, wmix_words
                 first = half * HALF + piece * P
                 nc.sync.dma_start(out[:, first : first + P].rearrange("(c p) j -> p c j", p=P), result[:])
 
-        gather_words(0, 0, "picked")
         gather_scales()
+        gather_words(0, 0, "picked")
         quantize_queries(0, 0, P, "first", 1)
         gather_words(1, 0, "picked")
         gather_words(0, 1, "first")

@@ -21,12 +21,15 @@ PACK = 4
 PASS = P * PACK
 K_PASSES = K // PASS
 R_PASSES = H // PASS
+PIECES = 4
 HALF = 512
 WORD_BYTES = 512 * T
 LIVE_ROWS = 100
 SPREAD_ROWS = 112
-STAGES = 4
-SCALAR_SHARE = 48
+SCALAR_SHARES = [[128, 128, 64, 48], [0, 0, 0, 0]]
+SQUARED_PIECES = [0, 1, 2, 3]
+SCALAR_PIECES = 3
+SQUARED = [(0, 1)]
 
 
 def tile_list_shortlist_relevance_mix_kernel(tc, tab, offs, wq, gain, wmix_words, wmix_scales, bias, out):
@@ -39,21 +42,21 @@ def tile_list_shortlist_relevance_mix_kernel(tc, tab, offs, wq, gain, wmix_words
         offsets = keep.tile([P, S // 16], U16, name="offsets")
         nc.sync.dma_start(offsets[:], offs)
 
-        tab_scales = keep.tile([P, T], U8, name="tab_scales", align_bytes=64)
-        nc.gpsimd.memset(tab_scales[:].bitcast(I32)[P // 2 :, :], 0)
+        tab_scales = keep.tile([P, T], U8, name="tab_scales", tag="stage1", align_bytes=64)
+        nc.vector.memset(tab_scales[:].bitcast(I32)[P // 2 :, :], 0)
         for m in range(2):
             rows = tab[m, WORD_BYTES:].rearrange("(h q x) -> q h x", h=2, q=16)
             nc.sync.dma_start(tab_scales[:].bitcast(I32)[m : P // 2 : 2, :], rows.bitcast(I32))
 
         def load_table_words(m):
-            words = keep.tile([P, T], I32, name="tab_words%d" % m, align_bytes=64)
+            words = keep.tile([P, T], I32, name="tab_words%d" % m, tag="stage%d" % (2 + 2 * m), align_bytes=64)
             nc.sync.dma_start(words[:], tab[m, :WORD_BYTES].rearrange("(p x) -> p x", p=P).bitcast(I32))
             return words
 
         staged = {}
 
         def load_queries(b, a):
-            staged[b, a] = work.tile([P, PACK, PASS], F32, name="raw", bufs=STAGES, align_bytes=64)
+            staged[b, a] = keep.tile([P, PACK, PASS], F32, name="raw%d%d" % (b, a), tag="stage%d" % a, align_bytes=64)
             rows = wq[a * PASS : (a + 1) * PASS, b * PASS : (b + 1) * PASS]
             nc.sync.dma_start(staged[b, a][:], rows.rearrange("(p i) c -> p i c", i=PACK))
 
@@ -67,30 +70,32 @@ def tile_list_shortlist_relevance_mix_kernel(tc, tab, offs, wq, gain, wmix_words
         load_queries(0, 0)
         tab_words.append(load_table_words(1))
         gains = keep.tile([P, R_PASSES, PACK], F32, name="gains")
-        nc.sync.dma_start(gains[:], gain.rearrange("(b p t) -> p b t", b=R_PASSES, t=PACK))
+        nc.gpsimd.dma_start(gains[:], gain.rearrange("(b p t) -> p b t", b=R_PASSES, t=PACK))
+
+        mix_scales = keep.tile([P, R_PASSES, N], U8, name="mix_scales", align_bytes=64)
+        nc.vector.memset(mix_scales[:].bitcast(I32), 0)
+        for quad in range(4):
+            nc.gpsimd.dma_start(
+                mix_scales[:].bitcast(I32)[32 * quad : 32 * quad + 4, :, :],
+                wmix_scales[:, 4 * quad : 4 * quad + 4, :].rearrange("b r x -> r b x").bitcast(I32),
+            )
+        biases = keep.tile([P, N // P], F32, name="biases", align_bytes=64)
+        with nc.allow_non_contiguous_dma(reason="one bias value for each partition and output tile"):
+            nc.gpsimd.dma_start(biases[:], bias.rearrange("(c p) -> p c", p=P))
 
         def load_mix():
-            words = work.tile([P, R_PASSES, 2 * N], U8, name="mix_words", tag="raw", bufs=STAGES, align_bytes=64)
+            words = keep.tile([P, R_PASSES, 2 * N], U8, name="mix_words", tag="stage1", align_bytes=64)
             nc.sync.dma_start(words[:].bitcast(I32), wmix_words.rearrange("b p x -> p b x").bitcast(I32))
-            scales = work.tile([P, R_PASSES, N], U8, name="mix_scales", tag="raw", bufs=STAGES, align_bytes=64)
-            nc.gpsimd.memset(scales[:].bitcast(I32), 0)
-            for quad in range(4):
-                nc.sync.dma_start(
-                    scales[:].bitcast(I32)[32 * quad : 32 * quad + 4, :, :],
-                    wmix_scales[:, 4 * quad : 4 * quad + 4, :].rearrange("b r x -> r b x").bitcast(I32),
-                )
-            columns = work.tile([P, N // P], F32, name="biases", tag="raw", bufs=STAGES, align_bytes=64)
-            with nc.allow_non_contiguous_dma(reason="one bias value for each partition and output tile"):
-                nc.sync.dma_start(columns[:], bias.rearrange("(c p) -> p c", p=P))
-            return words, scales, columns
+            return words
 
         v_scales = keep.tile([P, K_PASSES, S], U8, name="v_scales", align_bytes=64)
-        nc.gpsimd.memset(v_scales[:].bitcast(I32), 0)
+        nc.vector.memset(v_scales[:].bitcast(I32), 0)
 
         v_words = {}
 
-        def gather_words(m, half, tag):
-            picked = work.tile([P, HALF], U32, name="picked", tag=tag, bufs=1, align_bytes=64)
+        def gather_words(m, half):
+            tag = "stage3" if (m, half) == (0, 1) else "picked%d%d" % (m, half)
+            picked = keep.tile([P, HALF], U32, name="picked%d%d" % (m, half), tag=tag, align_bytes=64)
             entries = slice(half * HALF // 16, (half + 1) * HALF // 16)
             nc.vector.tensor_copy(picked[:], tab_words[m][:].bitcast(U32).indirect(offsets[:, entries]))
             parted = keep.tile([P, 2, 2 * HALF], U8, name="parted%d%d" % (m, half), align_bytes=64)
@@ -109,8 +114,8 @@ def tile_list_shortlist_relevance_mix_kernel(tc, tab, offs, wq, gain, wmix_words
 
         q_codes, q_scales = {}, {}
 
-        def quantize_queries(b, a, scalar_share, tag="grouped", bufs=3):
-            grouped = work.tile([P, PACK * PASS], BF16, name="grouped", tag=tag, bufs=bufs, align_bytes=64)
+        def quantize_queries(b, a, scalar_share):
+            grouped = work.tile([P, PACK * PASS], BF16, name="grouped", bufs=3, align_bytes=64)
             if (b, a) not in staged:
                 load_queries(b, a)
             src = staged[b, a][:].rearrange("p i (u t) -> p u i t", t=PACK)
@@ -140,47 +145,79 @@ def tile_list_shortlist_relevance_mix_kernel(tc, tab, offs, wq, gain, wmix_words
             return banks
 
         pass_by_pass = [(a, t) for a in range(K_PASSES) for t in range(PACK)]
-        bank_by_bank = [(0, t) for t in range(PACK)] + [(a, t) for t in range(PACK) for a in (2, 3, 1)]
+        bank_by_bank = [(a, t) for t in range(PACK) for a in range(K_PASSES)]
 
-        def relevance(b, banks):
+        def relevance(b, half, banks):
+            squared = (b, half) in SQUARED
             root = work.tile([P, PACK, HALF], F32, name="root", bufs=3, align_bytes=64)
-            partial = work.tile([P, PACK, HALF], F32, name="partial", bufs=3, align_bytes=64)
+            partial = work.tile([P, PACK, HALF], BF16 if squared else F32, name="partial", bufs=3, align_bytes=64)
             for t in range(PACK):
                 size = work.tile([P, HALF], F32, name="size", bufs=3, align_bytes=64)
                 nc.scalar.activation(size[:], banks[t][:], ACT.Abs)
-                nc.scalar.activation(root[:, t, :], size[:], ACT.Abs_reciprocal_sqrt, bias=one[:])
+                if squared:
+                    first = work.tile([P, HALF], F32, name="first_root", bufs=2, align_bytes=64)
+                    nc.scalar.activation(first[:], size[:], ACT.Abs_reciprocal_sqrt, bias=one[:])
+                    nc.scalar.activation(root[:, t, :], first[:], ACT.Square)
+                else:
+                    nc.scalar.activation(root[:, t, :], size[:], ACT.Abs_reciprocal_sqrt, bias=one[:])
                 nc.vector.scalar_tensor_tensor(
                     partial[:, t, :], banks[t][:], gains[:, b, t : t + 1], root[:, t, :], ALU.mult, ALU.mult
                 )
-            return root, partial
+            return squared, root, partial
+
+        def interleave(rounded, squared, root, partial):
+            dst = rounded[:].rearrange("p (g e t) -> p g t e", e=4, t=PACK)
+            src = partial[:].rearrange("p t (g e) -> p g t e", e=4)
+            if squared:
+                nc.vector.tensor_copy(dst, src)
+            else:
+                nc.vector.tensor_tensor(dst, src, root[:].rearrange("p t (g e) -> p g t e", e=4), ALU.mult)
 
         h_codes, h_scales = {}, {}
 
-        def quantize_relevance(b, half, root, partial):
-            rounded = work.tile([P, PACK * HALF], BF16, name="rounded", align_bytes=64)
-            nc.vector.tensor_tensor(
-                rounded[:].rearrange("p (g e t) -> p g t e", e=4, t=PACK),
-                partial[:].rearrange("p t (g e) -> p g t e", e=4),
-                root[:].rearrange("p t (g e) -> p g t e", e=4),
-                ALU.mult,
-            )
+        def quantize_relevance(b, half, parts):
+            rounded = work.tile([P, PACK * HALF], BF16, name="rounded", bufs=1, align_bytes=64)
+            interleave(rounded, *parts)
             h_codes[b, half] = keep.tile([P, HALF], U32, name="h_codes%d%d" % (b, half), align_bytes=64)
             h_scales[b, half] = keep.tile([P, HALF], U8, name="h_scales%d%d" % (b, half), align_bytes=64)
             nc.vector.quantize_mx(h_codes[b, half][:].bitcast(FP8X4), h_scales[b, half][:], rounded[:])
 
-        def last_relevance(b, banks):
-            flat = keep.tile([P, PACK, HALF], BF16, name="flat", align_bytes=64)
-            for t in range(PACK):
-                size = work.tile([P, HALF], F32, name="size", bufs=3, align_bytes=64)
-                nc.scalar.activation(size[:], banks[t][:], ACT.Abs)
-                root = work.tile([P, HALF], F32, name="root_last", bufs=3, align_bytes=64)
+        def products_in_pieces(b, half):
+            banks = []
+            for piece in range(PIECES):
+                bank = psum.tile([P, PACK, P], F32, name="acc_piece", tag="bank%d" % (PACK * half + piece))
+                first = half * HALF + piece * P
+                for a in range(K_PASSES):
+                    for t in range(PACK):
+                        cols = slice(t * P, (t + 1) * P)
+                        nc.tensor.matmul_mx(
+                            bank[:, t, :],
+                            lhsT=q_codes[b, a][:, cols].bitcast(FP8X4),
+                            lhsT_scale=q_scales[b, a][:, cols],
+                            rhs=v_words[a, half][:, 2 * piece * P : 2 * (piece + 1) * P].bitcast(FP4X4),
+                            rhs_scale=v_scales[:, 2 * (a % 2) + a // 2, first : first + P],
+                            start=(a == 0 and t == 0),
+                            stop=(a == K_PASSES - 1 and t == PACK - 1),
+                        )
+                banks.append(bank)
+            return banks
+
+        def relevance_piece(b, squared, bank):
+            size = work.tile([P, PACK, P], F32, name="size", bufs=3, align_bytes=64)
+            nc.scalar.activation(size[:], bank[:], ACT.Abs)
+            root = work.tile([P, PACK, P], F32, name="root_piece", bufs=PIECES, align_bytes=64)
+            if squared:
+                first = work.tile([P, PACK, P], F32, name="first_root", bufs=2, align_bytes=64)
+                nc.scalar.activation(first[:], size[:], ACT.Abs_reciprocal_sqrt, bias=one[:])
+                nc.scalar.activation(root[:], first[:], ACT.Square)
+            else:
                 nc.scalar.activation(root[:], size[:], ACT.Abs_reciprocal_sqrt, bias=one[:])
-                inverse = work.tile([P, HALF], F32, name="inverse", bufs=PACK, align_bytes=64)
-                nc.scalar.activation(inverse[:], root[:], ACT.Square)
+            partial = work.tile([P, PACK, P], BF16 if squared else F32, name="partial_piece", bufs=PIECES, align_bytes=64)
+            for t in range(PACK):
                 nc.vector.scalar_tensor_tensor(
-                    flat[:, t, :], banks[t][:], gains[:, b, t : t + 1], inverse[:], ALU.mult, ALU.mult
+                    partial[:, t, :], bank[:, t, :], gains[:, b, t : t + 1], root[:, t, :], ALU.mult, ALU.mult
                 )
-            return flat
+            return squared, root, partial
 
         def mix(half):
             for c in range(N // P):
@@ -199,18 +236,19 @@ def tile_list_shortlist_relevance_mix_kernel(tc, tab, offs, wq, gain, wmix_words
                 nc.scalar.activation(result[:], bank[:], ACT.Identity, bias=biases[:, c : c + 1])
                 nc.sync.dma_start(out[c * P : (c + 1) * P, half * HALF : (half + 1) * HALF], result[:])
 
-        def mix_in_pieces(half, flat):
-            pieces = HALF // P
-            for piece in range(pieces):
+        def quantize_piece(b, piece, bank):
+            parts = relevance_piece(b, piece in SQUARED_PIECES, bank)
+            rounded = work.tile([P, PACK * P], BF16, name="rounded_piece", bufs=PIECES, align_bytes=64)
+            interleave(rounded, *parts)
+            codes = work.tile([P, P], U32, name="codes_piece", bufs=PIECES, align_bytes=64)
+            scales = work.tile([P, P], U8, name="scales_piece", bufs=PIECES, align_bytes=64)
+            nc.vector.quantize_mx(codes[:].bitcast(FP8X4), scales[:], rounded[:])
+            return codes, scales
+
+        def mix_in_pieces(half, quantized):
+            pieces = PIECES
+            for piece, (codes, scales) in enumerate(quantized):
                 cols = slice(piece * P, (piece + 1) * P)
-                rounded = work.tile([P, PACK * P], BF16, name="rounded_piece", bufs=pieces, align_bytes=64)
-                nc.vector.tensor_copy(
-                    rounded[:].rearrange("p (g e t) -> p g t e", e=4, t=PACK),
-                    flat[:, :, cols].rearrange("p t (g e) -> p g t e", e=4),
-                )
-                codes = work.tile([P, P], U32, name="codes_piece", bufs=pieces, align_bytes=64)
-                scales = work.tile([P, P], U8, name="scales_piece", bufs=pieces, align_bytes=64)
-                nc.vector.quantize_mx(codes[:].bitcast(FP8X4), scales[:], rounded[:])
                 operands = [(h_codes[0, half][:, cols], h_scales[0, half][:, cols]), (codes[:], scales[:])]
                 bank = psum.tile([P, N // P, P], F32, name="score_piece", tag="bank%d" % (PACK * half + piece))
                 result = work.tile([P, N // P, P], F32, name="result_piece", bufs=pieces, align_bytes=64)
@@ -225,7 +263,7 @@ def tile_list_shortlist_relevance_mix_kernel(tc, tab, offs, wq, gain, wmix_words
                             start=(b == 0 and c == 0),
                             stop=(b == R_PASSES - 1 and c == N // P - 1),
                         )
-                if piece < pieces - 1:
+                if piece < SCALAR_PIECES:
                     for c in range(N // P):
                         nc.scalar.activation(result[:, c, :], bank[:, c, :], ACT.Identity, bias=biases[:, c : c + 1])
                 else:
@@ -236,27 +274,27 @@ def tile_list_shortlist_relevance_mix_kernel(tc, tab, offs, wq, gain, wmix_words
                 nc.sync.dma_start(out[:, first : first + P].rearrange("(c p) j -> p c j", p=P), result[:])
 
         gather_scales()
-        gather_words(0, 0, "picked")
-        quantize_queries(0, 0, P, "first", 1)
-        gather_words(1, 0, "picked")
-        gather_words(0, 1, "first")
-        quantize_queries(0, 1, P)
-        quantize_queries(0, 2, SCALAR_SHARE)
-        quantize_queries(0, 3, SCALAR_SHARE, "last", 1)
+        gather_words(0, 0)
+        gather_words(0, 1)
+        quantize_queries(0, 0, SCALAR_SHARES[0][0])
+        gather_words(1, 0)
+        gather_words(1, 1)
+        for a in range(1, K_PASSES):
+            quantize_queries(0, a, SCALAR_SHARES[0][a])
         banks00 = products(0, 0, pass_by_pass)
-        gather_words(1, 1, "last")
-        banks01 = products(0, 1, bank_by_bank)
-        for a in range(K_PASSES):
-            quantize_queries(1, a, 0 if a < K_PASSES // 2 else SCALAR_SHARE)
-        parts00 = relevance(0, banks00)
-        parts01 = relevance(0, banks01)
-        mix_words, mix_scales, biases = load_mix()
-        banks10 = products(1, 0, pass_by_pass)
-        banks11 = products(1, 1, pass_by_pass)
-        parts10 = relevance(1, banks10)
-        quantize_relevance(0, 0, *parts00)
-        quantize_relevance(1, 0, *parts10)
-        flat11 = last_relevance(1, banks11)
-        quantize_relevance(0, 1, *parts01)
+        banks01 = products(0, 1, pass_by_pass)
+        quantize_queries(1, 0, SCALAR_SHARES[1][0])
+        parts00 = relevance(0, 0, banks00)
+        for a in range(1, K_PASSES):
+            quantize_queries(1, a, SCALAR_SHARES[1][a])
+        parts01 = relevance(0, 1, banks01)
+        mix_words = load_mix()
+        banks10 = products(1, 0, bank_by_bank)
+        banks11 = products_in_pieces(1, 1)
+        quantize_relevance(0, 0, parts00)
+        parts10 = relevance(1, 0, banks10)
+        quantize_relevance(1, 0, parts10)
+        quantize_relevance(0, 1, parts01)
+        quantized = [quantize_piece(1, piece, bank) for piece, bank in enumerate(banks11)]
         mix(0)
-        mix_in_pieces(1, flat11)
+        mix_in_pieces(1, quantized)

@@ -29,6 +29,7 @@ SPREAD_ROWS = 112
 SCALAR_SHARES = [[128, 128, 64, 48], [0, 0, 0, 0]]
 SQUARED_PIECES = [0, 1, 2, 3]
 SCALAR_PIECES = 3
+HELD = {(1, 2): "partial01", (1, 3): "rounded"}
 SQUARED = [(0, 1)]
 
 
@@ -69,8 +70,6 @@ def tile_list_shortlist_relevance_mix_kernel(tc, tab, offs, wq, gain, wmix_words
 
         load_queries(0, 0)
         tab_words.append(load_table_words(1))
-        gains = keep.tile([P, R_PASSES, PACK], F32, name="gains")
-        nc.gpsimd.dma_start(gains[:], gain.rearrange("(b p t) -> p b t", b=R_PASSES, t=PACK))
 
         mix_scales = keep.tile([P, R_PASSES, N], U8, name="mix_scales", align_bytes=64)
         nc.vector.memset(mix_scales[:].bitcast(I32), 0)
@@ -79,29 +78,28 @@ def tile_list_shortlist_relevance_mix_kernel(tc, tab, offs, wq, gain, wmix_words
                 mix_scales[:].bitcast(I32)[32 * quad : 32 * quad + 4, :, :],
                 wmix_scales[:, 4 * quad : 4 * quad + 4, :].rearrange("b r x -> r b x").bitcast(I32),
             )
-        biases = keep.tile([P, N // P], F32, name="biases", align_bytes=64)
-        with nc.allow_non_contiguous_dma(reason="one bias value for each partition and output tile"):
-            nc.gpsimd.dma_start(biases[:], bias.rearrange("(c p) -> p c", p=P))
 
         def load_mix():
             words = keep.tile([P, R_PASSES, 2 * N], U8, name="mix_words", tag="stage1", align_bytes=64)
             nc.sync.dma_start(words[:].bitcast(I32), wmix_words.rearrange("b p x -> p b x").bitcast(I32))
-            return words
+            columns = keep.tile([P, N // P], F32, name="biases", tag="stage2", align_bytes=64)
+            with nc.allow_non_contiguous_dma(reason="one bias value for each partition and output tile"):
+                nc.sync.dma_start(columns[:], bias.rearrange("(c p) -> p c", p=P))
+            return words, columns
 
         v_scales = keep.tile([P, K_PASSES, S], U8, name="v_scales", align_bytes=64)
         nc.vector.memset(v_scales[:].bitcast(I32), 0)
 
         v_words = {}
 
-        def gather_words(m, half):
-            tag = "stage3" if (m, half) == (0, 1) else "picked%d%d" % (m, half)
-            picked = keep.tile([P, HALF], U32, name="picked%d%d" % (m, half), tag=tag, align_bytes=64)
-            entries = slice(half * HALF // 16, (half + 1) * HALF // 16)
-            nc.vector.tensor_copy(picked[:], tab_words[m][:].bitcast(U32).indirect(offsets[:, entries]))
-            parted = keep.tile([P, 2, 2 * HALF], U8, name="parted%d%d" % (m, half), align_bytes=64)
+        def gather_words(m):
+            picked = keep.tile([P, S], U32, name="picked%d" % m, tag="stage%d" % (3 + 2 * m), align_bytes=64)
+            nc.vector.tensor_copy(picked[:], tab_words[m][:].bitcast(U32).indirect(offsets[:]))
+            parted = keep.tile([P, 2, 2 * S], U8, name="parted%d" % m, align_bytes=64)
             nc.vector.tensor_copy(parted[:].bitcast(U16), picked[:].bitcast(U16).rearrange("p (j h) -> p h j", h=2))
             for h in range(2):
-                v_words[2 * m + h, half] = parted[:, h, :]
+                for half in range(2):
+                    v_words[2 * m + h, half] = parted[:, h, 2 * half * HALF : 2 * (half + 1) * HALF]
 
         def gather_scales():
             picked = keep.tile([P, S], U8, name="picked_scales", align_bytes=64)
@@ -115,7 +113,10 @@ def tile_list_shortlist_relevance_mix_kernel(tc, tab, offs, wq, gain, wmix_words
         q_codes, q_scales = {}, {}
 
         def quantize_queries(b, a, scalar_share):
-            grouped = work.tile([P, PACK * PASS], BF16, name="grouped", bufs=3, align_bytes=64)
+            late = (b, a) in HELD
+            grouped = work.tile(
+                [P, PACK * PASS], BF16, name="grouped", tag=HELD.get((b, a), "grouped"), bufs=1 if late else 3, align_bytes=64
+            )
             if (b, a) not in staged:
                 load_queries(b, a)
             src = staged[b, a][:].rearrange("p i (u t) -> p u i t", t=PACK)
@@ -130,6 +131,7 @@ def tile_list_shortlist_relevance_mix_kernel(tc, tab, offs, wq, gain, wmix_words
 
         def products(b, half, order):
             banks = [psum.tile([P, HALF], F32, name="acc", tag="bank%d" % (PACK * half + t)) for t in range(PACK)]
+            first = {t: a for a, t in reversed(order)}
             last = {t: a for a, t in order}
             for a, t in order:
                 cols = slice(t * P, (t + 1) * P)
@@ -139,7 +141,7 @@ def tile_list_shortlist_relevance_mix_kernel(tc, tab, offs, wq, gain, wmix_words
                     lhsT_scale=q_scales[b, a][:, cols],
                     rhs=v_words[a, half].bitcast(FP4X4),
                     rhs_scale=v_scales[:, 2 * (a % 2) + a // 2, half * HALF : (half + 1) * HALF],
-                    start=(a == 0),
+                    start=(a == first[t]),
                     stop=(a == last[t]),
                 )
             return banks
@@ -150,7 +152,9 @@ def tile_list_shortlist_relevance_mix_kernel(tc, tab, offs, wq, gain, wmix_words
         def relevance(b, half, banks):
             squared = (b, half) in SQUARED
             root = work.tile([P, PACK, HALF], F32, name="root", bufs=3, align_bytes=64)
-            partial = work.tile([P, PACK, HALF], BF16 if squared else F32, name="partial", bufs=3, align_bytes=64)
+            partial = work.tile(
+                [P, PACK, HALF], BF16 if squared else F32, name="partial", tag="partial%d%d" % (b, half), bufs=1, align_bytes=64
+            )
             for t in range(PACK):
                 size = work.tile([P, HALF], F32, name="size", bufs=3, align_bytes=64)
                 nc.scalar.activation(size[:], banks[t][:], ACT.Abs)
@@ -274,21 +278,21 @@ def tile_list_shortlist_relevance_mix_kernel(tc, tab, offs, wq, gain, wmix_words
                 nc.sync.dma_start(out[:, first : first + P].rearrange("(c p) j -> p c j", p=P), result[:])
 
         gather_scales()
-        gather_words(0, 0)
-        gather_words(0, 1)
+        gather_words(0)
         quantize_queries(0, 0, SCALAR_SHARES[0][0])
-        gather_words(1, 0)
-        gather_words(1, 1)
+        gather_words(1)
+        gains = keep.tile([P, R_PASSES, PACK], F32, name="gains", tag="stage4", align_bytes=64)
+        nc.sync.dma_start(gains[:], gain.rearrange("(b p t) -> p b t", b=R_PASSES, t=PACK))
         for a in range(1, K_PASSES):
             quantize_queries(0, a, SCALAR_SHARES[0][a])
         banks00 = products(0, 0, pass_by_pass)
-        banks01 = products(0, 1, pass_by_pass)
+        banks01 = products(0, 1, [(a, t) for t in range(PACK) for a in reversed(range(K_PASSES))])
         quantize_queries(1, 0, SCALAR_SHARES[1][0])
         parts00 = relevance(0, 0, banks00)
         for a in range(1, K_PASSES):
             quantize_queries(1, a, SCALAR_SHARES[1][a])
         parts01 = relevance(0, 1, banks01)
-        mix_words = load_mix()
+        mix_words, biases = load_mix()
         banks10 = products(1, 0, bank_by_bank)
         banks11 = products_in_pieces(1, 1)
         quantize_relevance(0, 0, parts00)

@@ -26,7 +26,8 @@ HALF = 512
 WORD_BYTES = 512 * T
 LIVE_ROWS = 100
 SPREAD_ROWS = 112
-SCALAR_SHARES = [[128, 128, 64, 48], [0, 0, 0, 0]]
+SCALAR_SHARES = [[128, 128, 64, 88], [0, 0, 0, 0]]
+HALVED = [(0, 3), (1, 0)]
 SQUARED_PIECES = [0, 1, 2, 3]
 SCALAR_PIECES = 3
 HELD = {(1, 2): "partial01", (1, 3): "rounded"}
@@ -57,9 +58,14 @@ def tile_list_shortlist_relevance_mix_kernel(tc, tab, offs, wq, gain, wmix_words
         staged = {}
 
         def load_queries(b, a):
-            staged[b, a] = keep.tile([P, PACK, PASS], F32, name="raw%d%d" % (b, a), tag="stage%d" % a, align_bytes=64)
-            rows = wq[a * PASS : (a + 1) * PASS, b * PASS : (b + 1) * PASS]
-            nc.sync.dma_start(staged[b, a][:], rows.rearrange("(p i) c -> p i c", i=PACK))
+            parts = 2 if (b, a) in HALVED else 1
+            width = PASS // parts
+            whole = keep.tile([P, parts, PACK, width], F32, name="raw%d%d" % (b, a), tag="stage%d" % a, align_bytes=64)
+            staged[b, a] = [whole[:, part] for part in range(parts)]
+            for part in range(parts):
+                first = b * PASS + part * width
+                rows = wq[a * PASS : (a + 1) * PASS, first : first + width]
+                nc.sync.dma_start(staged[b, a][part], rows.rearrange("(p i) c -> p i c", i=PACK))
 
         tab_words = [load_table_words(0)]
 
@@ -71,13 +77,6 @@ def tile_list_shortlist_relevance_mix_kernel(tc, tab, offs, wq, gain, wmix_words
         load_queries(0, 0)
         tab_words.append(load_table_words(1))
 
-        mix_scales = keep.tile([P, R_PASSES, N], U8, name="mix_scales", align_bytes=64)
-        nc.vector.memset(mix_scales[:].bitcast(I32), 0)
-        for quad in range(4):
-            nc.gpsimd.dma_start(
-                mix_scales[:].bitcast(I32)[32 * quad : 32 * quad + 4, :, :],
-                wmix_scales[:, 4 * quad : 4 * quad + 4, :].rearrange("b r x -> r b x").bitcast(I32),
-            )
 
         def load_mix():
             words = keep.tile([P, R_PASSES, 2 * N], U8, name="mix_words", tag="stage1", align_bytes=64)
@@ -85,10 +84,15 @@ def tile_list_shortlist_relevance_mix_kernel(tc, tab, offs, wq, gain, wmix_words
             columns = keep.tile([P, N // P], F32, name="biases", tag="stage2", align_bytes=64)
             with nc.allow_non_contiguous_dma(reason="one bias value for each partition and output tile"):
                 nc.sync.dma_start(columns[:], bias.rearrange("(c p) -> p c", p=P))
-            return words, columns
+            scales = keep.tile([P, R_PASSES, N], U8, name="mix_scales", tag="stage0", align_bytes=64)
+            for quad in range(4):
+                nc.sync.dma_start(
+                    scales[:].bitcast(I32)[32 * quad : 32 * quad + 4, :, :],
+                    wmix_scales[:, 4 * quad : 4 * quad + 4, :].rearrange("b r x -> r b x").bitcast(I32),
+                )
+            return words, scales, columns
 
         v_scales = keep.tile([P, K_PASSES, S], U8, name="v_scales", align_bytes=64)
-        nc.vector.memset(v_scales[:].bitcast(I32), 0)
 
         v_words = {}
 
@@ -119,15 +123,27 @@ def tile_list_shortlist_relevance_mix_kernel(tc, tab, offs, wq, gain, wmix_words
             )
             if (b, a) not in staged:
                 load_queries(b, a)
-            src = staged[b, a][:].rearrange("p i (u t) -> p u i t", t=PACK)
             dst = grouped[:].rearrange("p (t u i) -> p u i t", t=PACK, i=PACK)
             q_codes[b, a] = keep.tile([P, PASS], U32, name="q_codes%d%d" % (b, a), align_bytes=64)
             q_scales[b, a] = keep.tile([P, PASS], U8, name="q_scales%d%d" % (b, a), align_bytes=64)
-            if scalar_share > 0:
-                nc.scalar.copy(dst[:, :scalar_share], src[:, :scalar_share])
-            if scalar_share < P:
-                nc.vector.tensor_copy(dst[:, scalar_share:], src[:, scalar_share:])
-            nc.vector.quantize_mx(q_codes[b, a][:].bitcast(FP8X4), q_scales[b, a][:], grouped[:])
+            groups = P // len(staged[b, a])
+            for part, raw in enumerate(staged[b, a]):
+                src = raw.rearrange("p i (u t) -> p u i t", t=PACK)
+                first = part * groups
+                cut = min(max(scalar_share - first, 0), groups)
+                if cut > 0:
+                    nc.scalar.copy(dst[:, first : first + cut], src[:, :cut])
+                if cut < groups:
+                    nc.vector.tensor_copy(dst[:, first + cut : first + groups], src[:, cut:])
+            parts = PACK if (b, a) == (0, K_PASSES - 1) else 1
+            step = PASS // parts
+            for part in range(parts):
+                cols = slice(part * step, (part + 1) * step)
+                nc.vector.quantize_mx(
+                    q_codes[b, a][:, cols].bitcast(FP8X4),
+                    q_scales[b, a][:, cols],
+                    grouped[:, PACK * part * step : PACK * (part + 1) * step],
+                )
 
         def products(b, half, order):
             banks = [psum.tile([P, HALF], F32, name="acc", tag="bank%d" % (PACK * half + t)) for t in range(PACK)]
@@ -292,7 +308,7 @@ def tile_list_shortlist_relevance_mix_kernel(tc, tab, offs, wq, gain, wmix_words
         for a in range(1, K_PASSES):
             quantize_queries(1, a, SCALAR_SHARES[1][a])
         parts01 = relevance(0, 1, banks01)
-        mix_words, biases = load_mix()
+        mix_words, mix_scales, biases = load_mix()
         banks10 = products(1, 0, bank_by_bank)
         banks11 = products_in_pieces(1, 1)
         quantize_relevance(0, 0, parts00)

@@ -26,7 +26,7 @@ HALF = 512
 WORD_BYTES = 512 * T
 LIVE_ROWS = 100
 SPREAD_ROWS = 112
-SCALAR_SHARES = [[128, 128, 64, 88], [0, 0, 0, 0]]
+SCALAR_SHARES = [[128, 128, 64, 88], [0, 0, 0, 48]]
 HALVED = [(0, 3), (1, 0)]
 SQUARED_PIECES = [0, 1, 2, 3]
 SCALAR_PIECES = 3

@@ -28,10 +28,8 @@ LIVE_ROWS = 100
 SPREAD_ROWS = 112
 SCALAR_SHARES = [[128, 128, 64, 88], [0, 0, 0, 48]]
 HALVED = [(0, 3), (1, 0)]
-SQUARED_PIECES = [0, 1, 2, 3]
 SCALAR_PIECES = 3
 HELD = {(1, 2): "partial01", (1, 3): "rounded"}
-SQUARED = [(0, 1)]
 
 
 def tile_list_shortlist_relevance_mix_kernel(tc, tab, offs, wq, gain, wmix_words, wmix_scales, bias, out):
@@ -116,7 +114,8 @@ def tile_list_shortlist_relevance_mix_kernel(tc, tab, offs, wq, gain, wmix_words
 
         q_codes, q_scales = {}, {}
 
-        def quantize_queries(b, a, scalar_share):
+        def round_queries(b, a):
+            scalar_share = SCALAR_SHARES[b][a]
             late = (b, a) in HELD
             grouped = work.tile(
                 [P, PACK * PASS], BF16, name="grouped", tag=HELD.get((b, a), "grouped"), bufs=1 if late else 3, align_bytes=64
@@ -124,8 +123,6 @@ def tile_list_shortlist_relevance_mix_kernel(tc, tab, offs, wq, gain, wmix_words
             if (b, a) not in staged:
                 load_queries(b, a)
             dst = grouped[:].rearrange("p (t u i) -> p u i t", t=PACK, i=PACK)
-            q_codes[b, a] = keep.tile([P, PASS], U32, name="q_codes%d%d" % (b, a), align_bytes=64)
-            q_scales[b, a] = keep.tile([P, PASS], U8, name="q_scales%d%d" % (b, a), align_bytes=64)
             groups = P // len(staged[b, a])
             for part, raw in enumerate(staged[b, a]):
                 src = raw.rearrange("p i (u t) -> p u i t", t=PACK)
@@ -135,6 +132,11 @@ def tile_list_shortlist_relevance_mix_kernel(tc, tab, offs, wq, gain, wmix_words
                     nc.scalar.copy(dst[:, first : first + cut], src[:, :cut])
                 if cut < groups:
                     nc.vector.tensor_copy(dst[:, first + cut : first + groups], src[:, cut:])
+            return grouped
+
+        def quantize_queries(b, a, grouped):
+            q_codes[b, a] = keep.tile([P, PASS], U32, name="q_codes%d%d" % (b, a), align_bytes=64)
+            q_scales[b, a] = keep.tile([P, PASS], U8, name="q_scales%d%d" % (b, a), align_bytes=64)
             parts = PACK if (b, a) == (0, K_PASSES - 1) else 1
             step = PASS // parts
             for part in range(parts):
@@ -165,42 +167,51 @@ def tile_list_shortlist_relevance_mix_kernel(tc, tab, offs, wq, gain, wmix_words
         pass_by_pass = [(a, t) for a in range(K_PASSES) for t in range(PACK)]
         bank_by_bank = [(a, t) for t in range(PACK) for a in range(K_PASSES)]
 
-        def relevance(b, half, banks):
-            squared = (b, half) in SQUARED
-            root = work.tile([P, PACK, HALF], F32, name="root", bufs=3, align_bytes=64)
-            partial = work.tile(
-                [P, PACK, HALF], BF16 if squared else F32, name="partial", tag="partial%d%d" % (b, half), bufs=1, align_bytes=64
-            )
-            for t in range(PACK):
-                size = work.tile([P, HALF], F32, name="size", bufs=3, align_bytes=64)
-                nc.scalar.activation(size[:], banks[t][:], ACT.Abs)
-                if squared:
-                    first = work.tile([P, HALF], F32, name="first_root", bufs=2, align_bytes=64)
-                    nc.scalar.activation(first[:], size[:], ACT.Abs_reciprocal_sqrt, bias=one[:])
-                    nc.scalar.activation(root[:, t, :], first[:], ACT.Square)
-                else:
-                    nc.scalar.activation(root[:, t, :], size[:], ACT.Abs_reciprocal_sqrt, bias=one[:])
-                nc.vector.scalar_tensor_tensor(
-                    partial[:, t, :], banks[t][:], gains[:, b, t : t + 1], root[:, t, :], ALU.mult, ALU.mult
-                )
-            return squared, root, partial
-
-        def interleave(rounded, squared, root, partial):
-            dst = rounded[:].rearrange("p (g e t) -> p g t e", e=4, t=PACK)
-            src = partial[:].rearrange("p t (g e) -> p g t e", e=4)
+        def roots(squared, bank, root):
+            size = work.tile(list(root.shape), F32, name="size", bufs=3, align_bytes=64)
+            nc.scalar.activation(size[:], bank[:], ACT.Abs)
             if squared:
+                first = work.tile(list(root.shape), F32, name="first_root", bufs=2, align_bytes=64)
+                nc.scalar.activation(first[:], size[:], ACT.Abs_reciprocal_sqrt, bias=one[:])
+                nc.scalar.activation(root, first[:], ACT.Square)
+            else:
+                nc.scalar.activation(root, size[:], ACT.Abs_reciprocal_sqrt, bias=one[:])
+
+        def open_unit(b, squared, sums, banks, name, tag):
+            width = sums[0].shape[1]
+            root = work.tile([P, PACK, width], F32, name="root" + name, bufs=1, align_bytes=64)
+            tiles = PACK // len(banks)
+            for n, bank in enumerate(banks):
+                roots(squared, bank, root[:, n] if tiles == 1 else root[:])
+            partial = work.tile([P, PACK, width], BF16 if squared else F32, name="partial" + name, tag=tag, bufs=1, align_bytes=64)
+            return {"b": b, "squared": squared, "sums": sums, "root": root, "partial": partial, "width": width, "name": name}
+
+        def weigh(unit, tiles):
+            for t in tiles:
+                nc.vector.scalar_tensor_tensor(
+                    unit["partial"][:, t, :],
+                    unit["sums"][t],
+                    gains[:, unit["b"], t : t + 1],
+                    unit["root"][:, t, :],
+                    ALU.mult,
+                    ALU.mult,
+                )
+
+        def interleave(unit, tag):
+            rounded = work.tile([P, PACK * unit["width"]], BF16, name="rounded" + unit["name"], tag=tag, bufs=1, align_bytes=64)
+            dst = rounded[:].rearrange("p (g e t) -> p g t e", e=4, t=PACK)
+            src = unit["partial"][:].rearrange("p t (g e) -> p g t e", e=4)
+            if unit["squared"]:
                 nc.vector.tensor_copy(dst, src)
             else:
-                nc.vector.tensor_tensor(dst, src, root[:].rearrange("p t (g e) -> p g t e", e=4), ALU.mult)
+                nc.vector.tensor_tensor(dst, src, unit["root"][:].rearrange("p t (g e) -> p g t e", e=4), ALU.mult)
+            return rounded
 
-        h_codes, h_scales = {}, {}
-
-        def quantize_relevance(b, half, parts):
-            rounded = work.tile([P, PACK * HALF], BF16, name="rounded", bufs=1, align_bytes=64)
-            interleave(rounded, *parts)
-            h_codes[b, half] = keep.tile([P, HALF], U32, name="h_codes%d%d" % (b, half), align_bytes=64)
-            h_scales[b, half] = keep.tile([P, HALF], U8, name="h_scales%d%d" % (b, half), align_bytes=64)
-            nc.vector.quantize_mx(h_codes[b, half][:].bitcast(FP8X4), h_scales[b, half][:], rounded[:])
+        def quantize_relevance(unit, rounded):
+            codes = keep.tile([P, unit["width"]], U32, name="h_codes" + unit["name"], align_bytes=64)
+            scales = keep.tile([P, unit["width"]], U8, name="h_scales" + unit["name"], align_bytes=64)
+            nc.vector.quantize_mx(codes[:].bitcast(FP8X4), scales[:], rounded[:])
+            return codes, scales
 
         def products_in_pieces(b, half):
             banks = []
@@ -222,23 +233,6 @@ def tile_list_shortlist_relevance_mix_kernel(tc, tab, offs, wq, gain, wmix_words
                 banks.append(bank)
             return banks
 
-        def relevance_piece(b, squared, bank):
-            size = work.tile([P, PACK, P], F32, name="size", bufs=3, align_bytes=64)
-            nc.scalar.activation(size[:], bank[:], ACT.Abs)
-            root = work.tile([P, PACK, P], F32, name="root_piece", bufs=PIECES, align_bytes=64)
-            if squared:
-                first = work.tile([P, PACK, P], F32, name="first_root", bufs=2, align_bytes=64)
-                nc.scalar.activation(first[:], size[:], ACT.Abs_reciprocal_sqrt, bias=one[:])
-                nc.scalar.activation(root[:], first[:], ACT.Square)
-            else:
-                nc.scalar.activation(root[:], size[:], ACT.Abs_reciprocal_sqrt, bias=one[:])
-            partial = work.tile([P, PACK, P], BF16 if squared else F32, name="partial_piece", bufs=PIECES, align_bytes=64)
-            for t in range(PACK):
-                nc.vector.scalar_tensor_tensor(
-                    partial[:, t, :], bank[:, t, :], gains[:, b, t : t + 1], root[:, t, :], ALU.mult, ALU.mult
-                )
-            return squared, root, partial
-
         def mix(half):
             for c in range(N // P):
                 bank = psum.tile([P, HALF], F32, name="score", tag="bank%d" % (PACK * half + c))
@@ -247,8 +241,8 @@ def tile_list_shortlist_relevance_mix_kernel(tc, tab, offs, wq, gain, wmix_words
                         bank[:],
                         lhsT=mix_words[:, b, 2 * c * P : 2 * (c + 1) * P].bitcast(FP4X4),
                         lhsT_scale=mix_scales[:, b, c * P : (c + 1) * P],
-                        rhs=h_codes[b, half][:].bitcast(FP8X4),
-                        rhs_scale=h_scales[b, half][:],
+                        rhs=whole[b, half][0][:].bitcast(FP8X4),
+                        rhs_scale=whole[b, half][1][:],
                         start=(b == 0),
                         stop=(b == R_PASSES - 1),
                     )
@@ -256,20 +250,11 @@ def tile_list_shortlist_relevance_mix_kernel(tc, tab, offs, wq, gain, wmix_words
                 nc.scalar.activation(result[:], bank[:], ACT.Identity, bias=biases[:, c : c + 1])
                 nc.sync.dma_start(out[c * P : (c + 1) * P, half * HALF : (half + 1) * HALF], result[:])
 
-        def quantize_piece(b, piece, bank):
-            parts = relevance_piece(b, piece in SQUARED_PIECES, bank)
-            rounded = work.tile([P, PACK * P], BF16, name="rounded_piece", bufs=PIECES, align_bytes=64)
-            interleave(rounded, *parts)
-            codes = work.tile([P, P], U32, name="codes_piece", bufs=PIECES, align_bytes=64)
-            scales = work.tile([P, P], U8, name="scales_piece", bufs=PIECES, align_bytes=64)
-            nc.vector.quantize_mx(codes[:].bitcast(FP8X4), scales[:], rounded[:])
-            return codes, scales
-
         def mix_in_pieces(half, quantized):
             pieces = PIECES
             for piece, (codes, scales) in enumerate(quantized):
                 cols = slice(piece * P, (piece + 1) * P)
-                operands = [(h_codes[0, half][:, cols], h_scales[0, half][:, cols]), (codes[:], scales[:])]
+                operands = [(whole[0, half][0][:, cols], whole[0, half][1][:, cols]), (codes[:], scales[:])]
                 bank = psum.tile([P, N // P, P], F32, name="score_piece", tag="bank%d" % (PACK * half + piece))
                 result = work.tile([P, N // P, P], F32, name="result_piece", bufs=pieces, align_bytes=64)
                 for b in range(R_PASSES):
@@ -295,26 +280,61 @@ def tile_list_shortlist_relevance_mix_kernel(tc, tab, offs, wq, gain, wmix_words
 
         gather_scales()
         gather_words(0)
-        quantize_queries(0, 0, SCALAR_SHARES[0][0])
+        quantize_queries(0, 0, round_queries(0, 0))
         gather_words(1)
         gains = keep.tile([P, R_PASSES, PACK], F32, name="gains", tag="stage4", align_bytes=64)
         nc.sync.dma_start(gains[:], gain.rearrange("(b p t) -> p b t", b=R_PASSES, t=PACK))
         for a in range(1, K_PASSES):
-            quantize_queries(0, a, SCALAR_SHARES[0][a])
+            quantize_queries(0, a, round_queries(0, a))
         banks00 = products(0, 0, pass_by_pass)
         banks01 = products(0, 1, [(a, t) for t in range(PACK) for a in reversed(range(K_PASSES))])
-        quantize_queries(1, 0, SCALAR_SHARES[1][0])
-        parts00 = relevance(0, 0, banks00)
-        for a in range(1, K_PASSES):
-            quantize_queries(1, a, SCALAR_SHARES[1][a])
-        parts01 = relevance(0, 1, banks01)
+        whole = {}
+        grouped10 = round_queries(1, 0)
+        unit00 = open_unit(0, False, [x[:] for x in banks00], banks00, "00", "partial00")
+        weigh(unit00, [0])
+        quantize_queries(1, 0, grouped10)
+        weigh(unit00, [1])
+        grouped11 = round_queries(1, 1)
+        weigh(unit00, [2])
+        quantize_queries(1, 1, grouped11)
+        grouped12 = round_queries(1, 2)
+        weigh(unit00, [3])
+        grouped13 = round_queries(1, 3)
+        quantize_queries(1, 2, grouped12)
+        quantize_queries(1, 3, grouped13)
+        unit01 = open_unit(0, True, [x[:] for x in banks01], banks01, "01", "partial01")
         mix_words, mix_scales, biases = load_mix()
+        weigh(unit01, [0, 1])
+        rounded00 = interleave(unit00, "rounded")
+        weigh(unit01, [2])
+        whole[0, 0] = quantize_relevance(unit00, rounded00)
+        weigh(unit01, [3])
         banks10 = products(1, 0, bank_by_bank)
         banks11 = products_in_pieces(1, 1)
-        quantize_relevance(0, 0, parts00)
-        parts10 = relevance(1, 0, banks10)
-        quantize_relevance(1, 0, parts10)
-        quantize_relevance(0, 1, parts01)
-        quantized = [quantize_piece(1, piece, bank) for piece, bank in enumerate(banks11)]
+        unit10 = open_unit(1, False, [x[:] for x in banks10], banks10, "10", "partial10")
+        weigh(unit10, range(PACK))
+        rounded10 = interleave(unit10, "rounded")
+        pieces = [
+            open_unit(1, True, [bank[:, t, :] for t in range(PACK)], [bank], "p%d" % n, "partial_p%d" % n)
+            for n, bank in enumerate(banks11)
+        ]
+        rounded, quantized = {}, []
+        weigh(pieces[0], [0, 1])
+        whole[1, 0] = quantize_relevance(unit10, rounded10)
+        rounded01 = interleave(unit01, "rounded")
+        weigh(pieces[0], [2, 3])
+        whole[0, 1] = quantize_relevance(unit01, rounded01)
+        weigh(pieces[1], range(PACK))
+        rounded[0] = interleave(pieces[0], "rounded_p0")
+        weigh(pieces[2], range(PACK))
+        quantized.append(quantize_relevance(pieces[0], rounded[0]))
+        rounded[1] = interleave(pieces[1], "rounded_p1")
+        weigh(pieces[3], [0, 1])
+        quantized.append(quantize_relevance(pieces[1], rounded[1]))
+        rounded[2] = interleave(pieces[2], "rounded_p2")
+        weigh(pieces[3], [2, 3])
+        quantized.append(quantize_relevance(pieces[2], rounded[2]))
+        rounded[3] = interleave(pieces[3], "rounded_p3")
+        quantized.append(quantize_relevance(pieces[3], rounded[3]))
         mix(0)
         mix_in_pieces(1, quantized)

@@ -197,6 +197,12 @@ def tile_list_shortlist_relevance_mix_kernel(tc, tab, offs, wq, gain, wmix_words
                     ALU.mult,
                 )
 
+        def interleave_on_gpsimd(unit):
+            rounded = work.tile([P, PACK * unit["width"]], BF16, name="rounded" + unit["name"], bufs=1, align_bytes=64)
+            dst = rounded[:].rearrange("p (j t) -> p j t", t=PACK)
+            nc.gpsimd.tensor_scalar(dst, unit["partial"][:].rearrange("p t j -> p j t"), 1.0, 0.0, ALU.mult, ALU.add)
+            return rounded
+
         def interleave(unit, tag):
             rounded = work.tile([P, PACK * unit["width"]], BF16, name="rounded" + unit["name"], tag=tag, bufs=1, align_bytes=64)
             dst = rounded[:].rearrange("p (g e t) -> p g t e", e=4, t=PACK)
@@ -207,8 +213,9 @@ def tile_list_shortlist_relevance_mix_kernel(tc, tab, offs, wq, gain, wmix_words
                 nc.vector.tensor_tensor(dst, src, unit["root"][:].rearrange("p t (g e) -> p g t e", e=4), ALU.mult)
             return rounded
 
-        def quantize_relevance(unit, rounded):
-            codes = keep.tile([P, unit["width"]], U32, name="h_codes" + unit["name"], align_bytes=64)
+        def quantize_relevance(unit, rounded, tag=None):
+            name = "h_codes" + unit["name"]
+            codes = work.tile([P, unit["width"]], U32, name=name, tag=tag or name, bufs=1, align_bytes=64)
             scales = keep.tile([P, unit["width"]], U8, name="h_scales" + unit["name"], align_bytes=64)
             nc.vector.quantize_mx(codes[:].bitcast(FP8X4), scales[:], rounded[:])
             return codes, scales
@@ -318,23 +325,11 @@ def tile_list_shortlist_relevance_mix_kernel(tc, tab, offs, wq, gain, wmix_words
             open_unit(1, True, [bank[:, t, :] for t in range(PACK)], [bank], "p%d" % n, "partial_p%d" % n)
             for n, bank in enumerate(banks11)
         ]
-        rounded, quantized = {}, []
-        weigh(pieces[0], [0, 1])
         whole[1, 0] = quantize_relevance(unit10, rounded10)
-        rounded01 = interleave(unit01, "rounded")
-        weigh(pieces[0], [2, 3])
-        whole[0, 1] = quantize_relevance(unit01, rounded01)
-        weigh(pieces[1], range(PACK))
-        rounded[0] = interleave(pieces[0], "rounded_p0")
-        weigh(pieces[2], range(PACK))
-        quantized.append(quantize_relevance(pieces[0], rounded[0]))
-        rounded[1] = interleave(pieces[1], "rounded_p1")
-        weigh(pieces[3], [0, 1])
-        quantized.append(quantize_relevance(pieces[1], rounded[1]))
-        rounded[2] = interleave(pieces[2], "rounded_p2")
-        weigh(pieces[3], [2, 3])
-        quantized.append(quantize_relevance(pieces[2], rounded[2]))
-        rounded[3] = interleave(pieces[3], "rounded_p3")
-        quantized.append(quantize_relevance(pieces[3], rounded[3]))
+        whole[0, 1] = quantize_relevance(unit01, interleave_on_gpsimd(unit01), "partial10")
+        quantized = []
+        for piece in pieces:
+            weigh(piece, range(PACK))
+            quantized.append(quantize_relevance(piece, interleave(piece, "rounded" + piece["name"])))
         mix(0)
         mix_in_pieces(1, quantized)

@@ -26,10 +26,10 @@ HALF = 512
 WORD_BYTES = 512 * T
 LIVE_ROWS = 100
 SPREAD_ROWS = 112
-SCALAR_SHARES = [[128, 128, 64, 88], [0, 0, 0, 48]]
+SCALAR_SHARES = [[128, 128, 64, 88], [0, 0, 0, 16]]
 HALVED = [(0, 3), (1, 0)]
 SCALAR_PIECES = 3
-HELD = {(1, 2): "partial01", (1, 3): "rounded"}
+UNIT_BYTES = 2 * PACK * HALF
 
 
 def tile_list_shortlist_relevance_mix_kernel(tc, tab, offs, wq, gain, wmix_words, wmix_scales, bias, out):
@@ -37,6 +37,7 @@ def tile_list_shortlist_relevance_mix_kernel(tc, tab, offs, wq, gain, wmix_words
     with ExitStack() as ctx:
         keep = ctx.enter_context(tc.tile_pool(name="keep", bufs=1))
         work = ctx.enter_context(tc.tile_pool(name="work", bufs=2))
+        late = ctx.enter_context(tc.tile_pool(name="late", bufs=1))
         psum = ctx.enter_context(tc.psum_pool(name="psum", bufs=1))
 
         offsets = keep.tile([P, S // 16], U16, name="offsets")
@@ -116,10 +117,10 @@ def tile_list_shortlist_relevance_mix_kernel(tc, tab, offs, wq, gain, wmix_words
 
         def round_queries(b, a):
             scalar_share = SCALAR_SHARES[b][a]
-            late = (b, a) in HELD
-            grouped = work.tile(
-                [P, PACK * PASS], BF16, name="grouped", tag=HELD.get((b, a), "grouped"), bufs=1 if late else 3, align_bytes=64
-            )
+            if (b, a) == (R_PASSES - 1, K_PASSES - 1):
+                grouped = late.tile([P, PACK * PASS], BF16, name="grouped_last", offset=UNIT_BYTES // 2, align_bytes=64)
+            else:
+                grouped = work.tile([P, PACK * PASS], BF16, name="grouped", bufs=3, align_bytes=64)
             if (b, a) not in staged:
                 load_queries(b, a)
             dst = grouped[:].rearrange("p (t u i) -> p u i t", t=PACK, i=PACK)
@@ -183,7 +184,10 @@ def tile_list_shortlist_relevance_mix_kernel(tc, tab, offs, wq, gain, wmix_words
             tiles = PACK // len(banks)
             for n, bank in enumerate(banks):
                 roots(squared, bank, root[:, n] if tiles == 1 else root[:])
-            partial = work.tile([P, PACK, width], BF16 if squared else F32, name="partial" + name, tag=tag, bufs=1, align_bytes=64)
+            if tag == "late":
+                partial = late.tile([P, PACK, width], BF16, name="partial" + name, offset=0, align_bytes=64)
+            else:
+                partial = work.tile([P, PACK, width], BF16 if squared else F32, name="partial" + name, bufs=1, align_bytes=64)
             return {"b": b, "squared": squared, "sums": sums, "root": root, "partial": partial, "width": width, "name": name}
 
         def weigh(unit, tiles):
@@ -204,7 +208,10 @@ def tile_list_shortlist_relevance_mix_kernel(tc, tab, offs, wq, gain, wmix_words
             return rounded
 
         def interleave(unit, tag):
-            rounded = work.tile([P, PACK * unit["width"]], BF16, name="rounded" + unit["name"], tag=tag, bufs=1, align_bytes=64)
+            if tag == "rounded":
+                rounded = late.tile([P, PACK * HALF], BF16, name="rounded" + unit["name"], offset=UNIT_BYTES, align_bytes=64)
+            else:
+                rounded = work.tile([P, PACK * unit["width"]], BF16, name="rounded" + unit["name"], bufs=1, align_bytes=64)
             dst = rounded[:].rearrange("p (g e t) -> p g t e", e=4, t=PACK)
             src = unit["partial"][:].rearrange("p t (g e) -> p g t e", e=4)
             if unit["squared"]:
@@ -296,20 +303,12 @@ def tile_list_shortlist_relevance_mix_kernel(tc, tab, offs, wq, gain, wmix_words
         banks00 = products(0, 0, pass_by_pass)
         banks01 = products(0, 1, [(a, t) for t in range(PACK) for a in reversed(range(K_PASSES))])
         whole = {}
-        grouped10 = round_queries(1, 0)
-        unit00 = open_unit(0, False, [x[:] for x in banks00], banks00, "00", "partial00")
-        weigh(unit00, [0])
-        quantize_queries(1, 0, grouped10)
-        weigh(unit00, [1])
-        grouped11 = round_queries(1, 1)
-        weigh(unit00, [2])
-        quantize_queries(1, 1, grouped11)
-        grouped12 = round_queries(1, 2)
-        weigh(unit00, [3])
-        grouped13 = round_queries(1, 3)
-        quantize_queries(1, 2, grouped12)
-        quantize_queries(1, 3, grouped13)
-        unit01 = open_unit(0, True, [x[:] for x in banks01], banks01, "01", "partial01")
+        quantize_queries(1, 0, round_queries(1, 0))
+        unit00 = open_unit(0, False, [x[:] for x in banks00], banks00, "00", None)
+        weigh(unit00, range(PACK))
+        for a in range(1, K_PASSES):
+            quantize_queries(1, a, round_queries(1, a))
+        unit01 = open_unit(0, True, [x[:] for x in banks01], banks01, "01", "late")
         mix_words, mix_scales, biases = load_mix()
         weigh(unit01, [0, 1])
         rounded00 = interleave(unit00, "rounded")

@@ -24,11 +24,10 @@ R_PASSES = H // PASS
 PIECES = 4
 HALF = 512
 WORD_BYTES = 512 * T
-LIVE_ROWS = 100
-SPREAD_ROWS = 112
+SCALE_BASE = 32
 SCALAR_SHARES = [[128, 128, 64, 88], [0, 0, 0, 16]]
 HALVED = [(0, 3), (1, 0)]
-SCALAR_PIECES = 3
+SCALAR_PIECES = 2
 UNIT_BYTES = 2 * PACK * HALF
 
 
@@ -44,10 +43,11 @@ def tile_list_shortlist_relevance_mix_kernel(tc, tab, offs, wq, gain, wmix_words
         nc.sync.dma_start(offsets[:], offs)
 
         tab_scales = keep.tile([P, T], U8, name="tab_scales", tag="stage1", align_bytes=64)
-        nc.vector.memset(tab_scales[:].bitcast(I32)[P // 2 :, :], 0)
+        nc.vector.memset(tab_scales[:].bitcast(I32)[:SCALE_BASE, :], 0)
+        nc.vector.memset(tab_scales[:].bitcast(I32)[P - SCALE_BASE :, :], 0)
         for m in range(2):
             rows = tab[m, WORD_BYTES:].rearrange("(h q x) -> q h x", h=2, q=16)
-            nc.sync.dma_start(tab_scales[:].bitcast(I32)[m : P // 2 : 2, :], rows.bitcast(I32))
+            nc.sync.dma_start(tab_scales[:].bitcast(I32)[SCALE_BASE + m : P - SCALE_BASE : 2, :], rows.bitcast(I32))
 
         def load_table_words(m):
             words = keep.tile([P, T], I32, name="tab_words%d" % m, tag="stage%d" % (2 + 2 * m), align_bytes=64)
@@ -107,10 +107,10 @@ def tile_list_shortlist_relevance_mix_kernel(tc, tab, offs, wq, gain, wmix_words
         def gather_scales():
             picked = keep.tile([P, S], U8, name="picked_scales", align_bytes=64)
             nc.vector.tensor_copy(picked[:], tab_scales[:].indirect(offsets[:]))
-            for quad in range(4):
+            for quad in (0, 2, 1, 3):
                 nc.scalar.dma_start(
                     v_scales[:].bitcast(I32)[32 * quad : 32 * quad + 4, :, :],
-                    picked[:].bitcast(I32)[16 * quad : 16 * quad + 16, :],
+                    picked[:].bitcast(I32)[SCALE_BASE + 16 * quad : SCALE_BASE + 16 * quad + 16, :],
                 )
 
         q_codes, q_scales = {}, {}
@@ -201,8 +201,8 @@ def tile_list_shortlist_relevance_mix_kernel(tc, tab, offs, wq, gain, wmix_words
                     ALU.mult,
                 )
 
-        def interleave_on_gpsimd(unit):
-            rounded = work.tile([P, PACK * unit["width"]], BF16, name="rounded" + unit["name"], bufs=1, align_bytes=64)
+        def interleave_on_gpsimd(unit, tag):
+            rounded = work.tile([P, PACK * unit["width"]], BF16, name="rounded" + unit["name"], tag=tag, bufs=1, align_bytes=64)
             dst = rounded[:].rearrange("p (j t) -> p j t", t=PACK)
             nc.gpsimd.tensor_scalar(dst, unit["partial"][:].rearrange("p t j -> p j t"), 1.0, 0.0, ALU.mult, ALU.add)
             return rounded
@@ -325,10 +325,16 @@ def tile_list_shortlist_relevance_mix_kernel(tc, tab, offs, wq, gain, wmix_words
             for n, bank in enumerate(banks11)
         ]
         whole[1, 0] = quantize_relevance(unit10, rounded10)
-        whole[0, 1] = quantize_relevance(unit01, interleave_on_gpsimd(unit01), "partial10")
-        quantized = []
-        for piece in pieces:
+        whole[0, 1] = quantize_relevance(unit01, interleave_on_gpsimd(unit01, "rounded01"), "partial10")
+        quantized, rounded = [], []
+        for n, piece in enumerate(pieces):
             weigh(piece, range(PACK))
-            quantized.append(quantize_relevance(piece, interleave(piece, "rounded" + piece["name"])))
+            if n < PIECES - 1:
+                rounded.append(interleave_on_gpsimd(piece, "rounded" + piece["name"]))
+            if n >= 2:
+                quantized.append(quantize_relevance(pieces[n - 2], rounded[n - 2]))
+        rounded.append(interleave(pieces[-1], "rounded_last"))
+        for n in range(PIECES - 2, PIECES):
+            quantized.append(quantize_relevance(pieces[n], rounded[n]))
         mix(0)
         mix_in_pieces(1, quantized)

@@ -27,6 +27,7 @@ WORD_BYTES = 512 * T
 SCALE_BASE = 32
 SCALAR_SHARES = [[128, 128, 64, 88], [0, 0, 0, 16]]
 HALVED = [(0, 3), (1, 0)]
+BY_PAIRS = [(1, 2), (1, 3)]
 SCALAR_PIECES = 2
 UNIT_BYTES = 2 * PACK * HALF
 
@@ -132,13 +133,15 @@ def tile_list_shortlist_relevance_mix_kernel(tc, tab, offs, wq, gain, wmix_words
                 if cut > 0:
                     nc.scalar.copy(dst[:, first : first + cut], src[:, :cut])
                 if cut < groups:
-                    nc.vector.tensor_copy(dst[:, first + cut : first + groups], src[:, cut:])
+                    step = PACK // 2 if (b, a) in BY_PAIRS else PACK
+                    for t in range(0, PACK, step):
+                        nc.vector.tensor_copy(dst[:, first + cut : first + groups, :, t : t + step], src[:, cut:, :, t : t + step])
             return grouped
 
         def quantize_queries(b, a, grouped):
             q_codes[b, a] = keep.tile([P, PASS], U32, name="q_codes%d%d" % (b, a), align_bytes=64)
             q_scales[b, a] = keep.tile([P, PASS], U8, name="q_scales%d%d" % (b, a), align_bytes=64)
-            parts = PACK if (b, a) == (0, K_PASSES - 1) else 1
+            parts = PACK if (b, a) == (0, K_PASSES - 1) else 2 if (b, a) in BY_PAIRS else 1
             step = PASS // parts
             for part in range(parts):
                 cols = slice(part * step, (part + 1) * step)
@@ -188,7 +191,7 @@ def tile_list_shortlist_relevance_mix_kernel(tc, tab, offs, wq, gain, wmix_words
                 partial = late.tile([P, PACK, width], BF16, name="partial" + name, offset=0, align_bytes=64)
             else:
                 partial = work.tile([P, PACK, width], BF16 if squared else F32, name="partial" + name, bufs=1, align_bytes=64)
-            return {"b": b, "squared": squared, "sums": sums, "root": root, "partial": partial, "width": width, "name": name}
+            return {"b": b, "squared": squared, "sums": sums, "root": root, "partial": partial, "width": width, "name": name, "parts": 2 if name == "10" else 1}
 
         def weigh(unit, tiles):
             for t in tiles:
@@ -217,14 +220,23 @@ def tile_list_shortlist_relevance_mix_kernel(tc, tab, offs, wq, gain, wmix_words
             if unit["squared"]:
                 nc.vector.tensor_copy(dst, src)
             else:
-                nc.vector.tensor_tensor(dst, src, unit["root"][:].rearrange("p t (g e) -> p g t e", e=4), ALU.mult)
+                root = unit["root"][:].rearrange("p t (g e) -> p g t e", e=4)
+                step = unit["width"] // 4 // unit["parts"]
+                for first in range(0, unit["width"] // 4, step):
+                    part = slice(first, first + step)
+                    nc.vector.tensor_tensor(dst[:, part], src[:, part], root[:, part], ALU.mult)
             return rounded
 
         def quantize_relevance(unit, rounded, tag=None):
             name = "h_codes" + unit["name"]
             codes = work.tile([P, unit["width"]], U32, name=name, tag=tag or name, bufs=1, align_bytes=64)
             scales = keep.tile([P, unit["width"]], U8, name="h_scales" + unit["name"], align_bytes=64)
-            nc.vector.quantize_mx(codes[:].bitcast(FP8X4), scales[:], rounded[:])
+            step = unit["width"] // unit["parts"]
+            for first in range(0, unit["width"], step):
+                cols = slice(first, first + step)
+                nc.vector.quantize_mx(
+                    codes[:, cols].bitcast(FP8X4), scales[:, cols], rounded[:, PACK * first : PACK * (first + step)]
+                )
             return codes, scales
 
         def products_in_pieces(b, half):

@@ -25,9 +25,8 @@ PIECES = 4
 HALF = 512
 WORD_BYTES = 512 * T
 SCALE_BASE = 32
-SCALAR_SHARES = [[128, 128, 64, 88], [0, 0, 0, 16]]
+SCALAR_SHARES = [[128, 128, 64, 88], [0, 0, 0, 0]]
 HALVED = [(0, 3), (1, 0)]
-BY_PAIRS = [(1, 2), (1, 3)]
 SCALAR_PIECES = 2
 UNIT_BYTES = 2 * PACK * HALF
 
@@ -118,12 +117,22 @@ def tile_list_shortlist_relevance_mix_kernel(tc, tab, offs, wq, gain, wmix_words
 
         def round_queries(b, a):
             scalar_share = SCALAR_SHARES[b][a]
-            if (b, a) == (R_PASSES - 1, K_PASSES - 1):
-                grouped = late.tile([P, PACK * PASS], BF16, name="grouped_last", offset=UNIT_BYTES // 2, align_bytes=64)
-            else:
-                grouped = work.tile([P, PACK * PASS], BF16, name="grouped", bufs=3, align_bytes=64)
             if (b, a) not in staged:
                 load_queries(b, a)
+            if (b, a) == (R_PASSES - 1, K_PASSES - 1):
+                src = staged[b, a][0].rearrange("p i (u t) -> p u i t", t=PACK)
+                pairs = []
+                for pair in range(2):
+                    offset = (pair + 1) * UNIT_BYTES // 2
+                    tile = late.tile([P, 2 * PASS], BF16, name="grouped_last%d" % pair, offset=offset, align_bytes=64)
+                    dst = tile[:].rearrange("p (t u i) -> p u i t", t=2, i=PACK)
+                    cut = 2 * scalar_share * pair
+                    if cut > 0:
+                        nc.scalar.copy(dst[:, :cut], src[:, :cut, :, 2 * pair : 2 * pair + 2])
+                    nc.vector.tensor_copy(dst[:, cut:], src[:, cut:, :, 2 * pair : 2 * pair + 2])
+                    pairs.append(tile[:])
+                return pairs
+            grouped = work.tile([P, PACK * PASS], BF16, name="grouped", bufs=3, align_bytes=64)
             dst = grouped[:].rearrange("p (t u i) -> p u i t", t=PACK, i=PACK)
             groups = P // len(staged[b, a])
             for part, raw in enumerate(staged[b, a]):
@@ -133,23 +142,20 @@ def tile_list_shortlist_relevance_mix_kernel(tc, tab, offs, wq, gain, wmix_words
                 if cut > 0:
                     nc.scalar.copy(dst[:, first : first + cut], src[:, :cut])
                 if cut < groups:
-                    step = PACK // 2 if (b, a) in BY_PAIRS else PACK
+                    step = PACK // 2 if (b == R_PASSES - 1 or a == K_PASSES - 1) and first + groups == P else PACK
                     for t in range(0, PACK, step):
                         nc.vector.tensor_copy(dst[:, first + cut : first + groups, :, t : t + step], src[:, cut:, :, t : t + step])
-            return grouped
+            parts = 2 if b == R_PASSES - 1 else PACK if a == K_PASSES - 1 else 1
+            step = PACK * PASS // parts
+            return [grouped[:, part * step : (part + 1) * step] for part in range(parts)]
 
         def quantize_queries(b, a, grouped):
             q_codes[b, a] = keep.tile([P, PASS], U32, name="q_codes%d%d" % (b, a), align_bytes=64)
             q_scales[b, a] = keep.tile([P, PASS], U8, name="q_scales%d%d" % (b, a), align_bytes=64)
-            parts = PACK if (b, a) == (0, K_PASSES - 1) else 2 if (b, a) in BY_PAIRS else 1
-            step = PASS // parts
-            for part in range(parts):
+            step = PASS // len(grouped)
+            for part, source in enumerate(grouped):
                 cols = slice(part * step, (part + 1) * step)
-                nc.vector.quantize_mx(
-                    q_codes[b, a][:, cols].bitcast(FP8X4),
-                    q_scales[b, a][:, cols],
-                    grouped[:, PACK * part * step : PACK * (part + 1) * step],
-                )
+                nc.vector.quantize_mx(q_codes[b, a][:, cols].bitcast(FP8X4), q_scales[b, a][:, cols], source)
 
         def products(b, half, order):
             banks = [psum.tile([P, HALF], F32, name="acc", tag="bank%d" % (PACK * half + t)) for t in range(PACK)]
@@ -195,14 +201,17 @@ def tile_list_shortlist_relevance_mix_kernel(tc, tab, offs, wq, gain, wmix_words
 
         def weigh(unit, tiles):
             for t in tiles:
-                nc.vector.scalar_tensor_tensor(
-                    unit["partial"][:, t, :],
-                    unit["sums"][t],
-                    gains[:, unit["b"], t : t + 1],
-                    unit["root"][:, t, :],
-                    ALU.mult,
-                    ALU.mult,
-                )
+                step = unit["width"] // (unit["parts"] if t == PACK - 1 else 1)
+                for first in range(0, unit["width"], step):
+                    cols = slice(first, first + step)
+                    nc.vector.scalar_tensor_tensor(
+                        unit["partial"][:, t, cols],
+                        unit["sums"][t][:, cols],
+                        gains[:, unit["b"], t : t + 1],
+                        unit["root"][:, t, cols],
+                        ALU.mult,
+                        ALU.mult,
+                    )
 
         def interleave_on_gpsimd(unit, tag):
             rounded = work.tile([P, PACK * unit["width"]], BF16, name="rounded" + unit["name"], tag=tag, bufs=1, align_bytes=64)

from contextlib import ExitStack

import concourse.mybir as mybir

K, T, S, H, N = 2048, 2048, 1024, 1024, 512
FLOPS = 2 * K * H * S + 2 * H * N * S

F32 = mybir.dt.float32
BF16 = mybir.dt.bfloat16
I32 = mybir.dt.int32
U32 = mybir.dt.uint32
U16 = mybir.dt.uint16
U8 = mybir.dt.uint8
FP8X4 = mybir.dt.float8_e4m3fn_x4
FP4X4 = mybir.dt.float4_e2m1fn_x4
ACT = mybir.ActivationFunctionType
ALU = mybir.AluOpType

P = 128
PACK = 4
PASS = P * PACK
K_PASSES = K // PASS
R_PASSES = H // PASS
PIECES = 4
HALF = 512
WORD_BYTES = 512 * T
SCALE_BASE = 32
SCALAR_SHARES = [[128, 128, 64, 88], [0, 0, 0, 0]]
HALVED = [(0, 3), (1, 0)]
SCALAR_PIECES = 2
UNIT_BYTES = 2 * PACK * HALF


def tile_list_shortlist_relevance_mix_kernel(tc, tab, offs, wq, gain, wmix_words, wmix_scales, bias, out):
    nc = tc.nc
    with ExitStack() as ctx:
        keep = ctx.enter_context(tc.tile_pool(name="keep", bufs=1))
        work = ctx.enter_context(tc.tile_pool(name="work", bufs=2))
        late = ctx.enter_context(tc.tile_pool(name="late", bufs=1))
        psum = ctx.enter_context(tc.psum_pool(name="psum", bufs=1))

        offsets = keep.tile([P, S // 16], U16, name="offsets")
        nc.sync.dma_start(offsets[:], offs)

        tab_scales = keep.tile([P, T], U8, name="tab_scales", tag="stage1", align_bytes=64)
        nc.vector.memset(tab_scales[:].bitcast(I32)[:SCALE_BASE, :], 0)
        nc.vector.memset(tab_scales[:].bitcast(I32)[P - SCALE_BASE :, :], 0)
        for m in range(2):
            rows = tab[m, WORD_BYTES:].rearrange("(h q x) -> q h x", h=2, q=16)
            nc.sync.dma_start(tab_scales[:].bitcast(I32)[SCALE_BASE + m : P - SCALE_BASE : 2, :], rows.bitcast(I32))

        def load_table_words(m):
            words = keep.tile([P, T], I32, name="tab_words%d" % m, tag="stage%d" % (2 + 2 * m), align_bytes=64)
            nc.sync.dma_start(words[:], tab[m, :WORD_BYTES].rearrange("(p x) -> p x", p=P).bitcast(I32))
            return words

        staged = {}

        def load_queries(b, a):
            parts = 2 if (b, a) in HALVED else 1
            width = PASS // parts
            whole = keep.tile([P, parts, PACK, width], F32, name="raw%d%d" % (b, a), tag="stage%d" % a, align_bytes=64)
            staged[b, a] = [whole[:, part] for part in range(parts)]
            for part in range(parts):
                first = b * PASS + part * width
                rows = wq[a * PASS : (a + 1) * PASS, first : first + width]
                nc.sync.dma_start(staged[b, a][part], rows.rearrange("(p i) c -> p i c", i=PACK))

        tab_words = [load_table_words(0)]

        one = keep.tile([P, 1], F32, name="one")
        nc.vector.memset(one[:], 1.0)
        warm = keep.tile([P, 1], F32, name="warm")
        nc.scalar.activation(warm[:], one[:], ACT.Abs_reciprocal_sqrt)

        load_queries(0, 0)
        tab_words.append(load_table_words(1))


        def load_mix():
            words = keep.tile([P, R_PASSES, 2 * N], U8, name="mix_words", tag="stage1", align_bytes=64)
            nc.sync.dma_start(words[:].bitcast(I32), wmix_words.rearrange("b p x -> p b x").bitcast(I32))
            columns = keep.tile([P, N // P], F32, name="biases", tag="stage2", align_bytes=64)
            with nc.allow_non_contiguous_dma(reason="one bias value for each partition and output tile"):
                nc.sync.dma_start(columns[:], bias.rearrange("(c p) -> p c", p=P))
            scales = keep.tile([P, R_PASSES, N], U8, name="mix_scales", tag="stage0", align_bytes=64)
            for quad in range(4):
                nc.sync.dma_start(
                    scales[:].bitcast(I32)[32 * quad : 32 * quad + 4, :, :],
                    wmix_scales[:, 4 * quad : 4 * quad + 4, :].rearrange("b r x -> r b x").bitcast(I32),
                )
            return words, scales, columns

        v_scales = keep.tile([P, K_PASSES, S], U8, name="v_scales", align_bytes=64)

        v_words = {}

        def gather_words(m):
            picked = keep.tile([P, S], U32, name="picked%d" % m, tag="stage%d" % (3 + 2 * m), align_bytes=64)
            nc.vector.tensor_copy(picked[:], tab_words[m][:].bitcast(U32).indirect(offsets[:]))
            parted = keep.tile([P, 2, 2 * S], U8, name="parted%d" % m, align_bytes=64)
            nc.vector.tensor_copy(parted[:].bitcast(U16), picked[:].bitcast(U16).rearrange("p (j h) -> p h j", h=2))
            for h in range(2):
                for half in range(2):
                    v_words[2 * m + h, half] = parted[:, h, 2 * half * HALF : 2 * (half + 1) * HALF]

        def gather_scales():
            picked = keep.tile([P, S], U8, name="picked_scales", align_bytes=64)
            nc.vector.tensor_copy(picked[:], tab_scales[:].indirect(offsets[:]))
            for quad in (0, 2, 1, 3):
                nc.scalar.dma_start(
                    v_scales[:].bitcast(I32)[32 * quad : 32 * quad + 4, :, :],
                    picked[:].bitcast(I32)[SCALE_BASE + 16 * quad : SCALE_BASE + 16 * quad + 16, :],
                )

        q_codes, q_scales = {}, {}

        def round_queries(b, a):
            scalar_share = SCALAR_SHARES[b][a]
            if (b, a) not in staged:
                load_queries(b, a)
            if (b, a) == (R_PASSES - 1, K_PASSES - 1):
                src = staged[b, a][0].rearrange("p i (u t) -> p u i t", t=PACK)
                pairs = []
                for pair in range(2):
                    offset = (pair + 1) * UNIT_BYTES // 2
                    tile = late.tile([P, 2 * PASS], BF16, name="grouped_last%d" % pair, offset=offset, align_bytes=64)
                    dst = tile[:].rearrange("p (t u i) -> p u i t", t=2, i=PACK)
                    cut = 2 * scalar_share * pair
                    if cut > 0:
                        nc.scalar.copy(dst[:, :cut], src[:, :cut, :, 2 * pair : 2 * pair + 2])
                    nc.vector.tensor_copy(dst[:, cut:], src[:, cut:, :, 2 * pair : 2 * pair + 2])
                    pairs.append(tile[:])
                return pairs
            grouped = work.tile([P, PACK * PASS], BF16, name="grouped", bufs=3, align_bytes=64)
            dst = grouped[:].rearrange("p (t u i) -> p u i t", t=PACK, i=PACK)
            groups = P // len(staged[b, a])
            for part, raw in enumerate(staged[b, a]):
                src = raw.rearrange("p i (u t) -> p u i t", t=PACK)
                first = part * groups
                cut = min(max(scalar_share - first, 0), groups)
                if cut > 0:
                    nc.scalar.copy(dst[:, first : first + cut], src[:, :cut])
                if cut < groups:
                    step = PACK // 2 if (b == R_PASSES - 1 or a == K_PASSES - 1) and first + groups == P else PACK
                    for t in range(0, PACK, step):
                        nc.vector.tensor_copy(dst[:, first + cut : first + groups, :, t : t + step], src[:, cut:, :, t : t + step])
            parts = 2 if b == R_PASSES - 1 else PACK if a == K_PASSES - 1 else 1
            step = PACK * PASS // parts
            return [grouped[:, part * step : (part + 1) * step] for part in range(parts)]

        def quantize_queries(b, a, grouped):
            q_codes[b, a] = keep.tile([P, PASS], U32, name="q_codes%d%d" % (b, a), align_bytes=64)
            q_scales[b, a] = keep.tile([P, PASS], U8, name="q_scales%d%d" % (b, a), align_bytes=64)
            step = PASS // len(grouped)
            for part, source in enumerate(grouped):
                cols = slice(part * step, (part + 1) * step)
                nc.vector.quantize_mx(q_codes[b, a][:, cols].bitcast(FP8X4), q_scales[b, a][:, cols], source)

        def products(b, half, order):
            banks = [psum.tile([P, HALF], F32, name="acc", tag="bank%d" % (PACK * half + t)) for t in range(PACK)]
            first = {t: a for a, t in reversed(order)}
            last = {t: a for a, t in order}
            for a, t in order:
                cols = slice(t * P, (t + 1) * P)
                nc.tensor.matmul_mx(
                    banks[t][:],
                    lhsT=q_codes[b, a][:, cols].bitcast(FP8X4),
                    lhsT_scale=q_scales[b, a][:, cols],
                    rhs=v_words[a, half].bitcast(FP4X4),
                    rhs_scale=v_scales[:, 2 * (a % 2) + a // 2, half * HALF : (half + 1) * HALF],
                    start=(a == first[t]),
                    stop=(a == last[t]),
                )
            return banks

        pass_by_pass = [(a, t) for a in range(K_PASSES) for t in range(PACK)]
        bank_by_bank = [(a, t) for t in range(PACK) for a in range(K_PASSES)]

        def roots(squared, bank, root):
            size = work.tile(list(root.shape), F32, name="size", bufs=3, align_bytes=64)
            nc.scalar.activation(size[:], bank[:], ACT.Abs)
            if squared:
                first = work.tile(list(root.shape), F32, name="first_root", bufs=2, align_bytes=64)
                nc.scalar.activation(first[:], size[:], ACT.Abs_reciprocal_sqrt, bias=one[:])
                nc.scalar.activation(root, first[:], ACT.Square)
            else:
                nc.scalar.activation(root, size[:], ACT.Abs_reciprocal_sqrt, bias=one[:])

        def open_unit(b, squared, sums, banks, name, tag):
            width = sums[0].shape[1]
            root = work.tile([P, PACK, width], F32, name="root" + name, bufs=1, align_bytes=64)
            tiles = PACK // len(banks)
            for n, bank in enumerate(banks):
                roots(squared, bank, root[:, n] if tiles == 1 else root[:])
            if tag == "late":
                partial = late.tile([P, PACK, width], BF16, name="partial" + name, offset=0, align_bytes=64)
            else:
                partial = work.tile([P, PACK, width], BF16 if squared else F32, name="partial" + name, bufs=1, align_bytes=64)
            return {"b": b, "squared": squared, "sums": sums, "root": root, "partial": partial, "width": width, "name": name, "parts": 2 if name == "10" else 1}

        def weigh(unit, tiles):
            for t in tiles:
                step = unit["width"] // (unit["parts"] if t == PACK - 1 else 1)
                for first in range(0, unit["width"], step):
                    cols = slice(first, first + step)
                    nc.vector.scalar_tensor_tensor(
                        unit["partial"][:, t, cols],
                        unit["sums"][t][:, cols],
                        gains[:, unit["b"], t : t + 1],
                        unit["root"][:, t, cols],
                        ALU.mult,
                        ALU.mult,
                    )

        def interleave_on_gpsimd(unit, tag):
            rounded = work.tile([P, PACK * unit["width"]], BF16, name="rounded" + unit["name"], tag=tag, bufs=1, align_bytes=64)
            dst = rounded[:].rearrange("p (j t) -> p j t", t=PACK)
            nc.gpsimd.tensor_scalar(dst, unit["partial"][:].rearrange("p t j -> p j t"), 1.0, 0.0, ALU.mult, ALU.add)
            return rounded

        def interleave(unit, tag):
            if tag == "rounded":
                rounded = late.tile([P, PACK * HALF], BF16, name="rounded" + unit["name"], offset=UNIT_BYTES, align_bytes=64)
            else:
                rounded = work.tile([P, PACK * unit["width"]], BF16, name="rounded" + unit["name"], bufs=1, align_bytes=64)
            dst = rounded[:].rearrange("p (g e t) -> p g t e", e=4, t=PACK)
            src = unit["partial"][:].rearrange("p t (g e) -> p g t e", e=4)
            if unit["squared"]:
                nc.vector.tensor_copy(dst, src)
            else:
                root = unit["root"][:].rearrange("p t (g e) -> p g t e", e=4)
                step = unit["width"] // 4 // unit["parts"]
                for first in range(0, unit["width"] // 4, step):
                    part = slice(first, first + step)
                    nc.vector.tensor_tensor(dst[:, part], src[:, part], root[:, part], ALU.mult)
            return rounded

        def quantize_relevance(unit, rounded, tag=None):
            name = "h_codes" + unit["name"]
            codes = work.tile([P, unit["width"]], U32, name=name, tag=tag or name, bufs=1, align_bytes=64)
            scales = keep.tile([P, unit["width"]], U8, name="h_scales" + unit["name"], align_bytes=64)
            step = unit["width"] // unit["parts"]
            for first in range(0, unit["width"], step):
                cols = slice(first, first + step)
                nc.vector.quantize_mx(
                    codes[:, cols].bitcast(FP8X4), scales[:, cols], rounded[:, PACK * first : PACK * (first + step)]
                )
            return codes, scales

        def products_in_pieces(b, half):
            banks = []
            for piece in range(PIECES):
                bank = psum.tile([P, PACK, P], F32, name="acc_piece", tag="bank%d" % (PACK * half + piece))
                first = half * HALF + piece * P
                for a in range(K_PASSES):
                    for t in range(PACK):
                        cols = slice(t * P, (t + 1) * P)
                        nc.tensor.matmul_mx(
                            bank[:, t, :],
                            lhsT=q_codes[b, a][:, cols].bitcast(FP8X4),
                            lhsT_scale=q_scales[b, a][:, cols],
                            rhs=v_words[a, half][:, 2 * piece * P : 2 * (piece + 1) * P].bitcast(FP4X4),
                            rhs_scale=v_scales[:, 2 * (a % 2) + a // 2, first : first + P],
                            start=(a == 0 and t == 0),
                            stop=(a == K_PASSES - 1 and t == PACK - 1),
                        )
                banks.append(bank)
            return banks

        def mix(half):
            for c in range(N // P):
                bank = psum.tile([P, HALF], F32, name="score", tag="bank%d" % (PACK * half + c))
                for b in range(R_PASSES):
                    nc.tensor.matmul_mx(
                        bank[:],
                        lhsT=mix_words[:, b, 2 * c * P : 2 * (c + 1) * P].bitcast(FP4X4),
                        lhsT_scale=mix_scales[:, b, c * P : (c + 1) * P],
                        rhs=whole[b, half][0][:].bitcast(FP8X4),
                        rhs_scale=whole[b, half][1][:],
                        start=(b == 0),
                        stop=(b == R_PASSES - 1),
                    )
                result = work.tile([P, HALF], F32, name="result", bufs=8, align_bytes=64)
                nc.scalar.activation(result[:], bank[:], ACT.Identity, bias=biases[:, c : c + 1])
                nc.sync.dma_start(out[c * P : (c + 1) * P, half * HALF : (half + 1) * HALF], result[:])

        def mix_in_pieces(half, quantized):
            pieces = PIECES
            for piece, (codes, scales) in enumerate(quantized):
                cols = slice(piece * P, (piece + 1) * P)
                operands = [(whole[0, half][0][:, cols], whole[0, half][1][:, cols]), (codes[:], scales[:])]
                bank = psum.tile([P, N // P, P], F32, name="score_piece", tag="bank%d" % (PACK * half + piece))
                result = work.tile([P, N // P, P], F32, name="result_piece", bufs=pieces, align_bytes=64)
                for b in range(R_PASSES):
                    for c in range(N // P):
                        nc.tensor.matmul_mx(
                            bank[:, c, :],
                            lhsT=mix_words[:, b, 2 * c * P : 2 * (c + 1) * P].bitcast(FP4X4),
                            lhsT_scale=mix_scales[:, b, c * P : (c + 1) * P],
                            rhs=operands[b][0].bitcast(FP8X4),
                            rhs_scale=operands[b][1],
                            start=(b == 0 and c == 0),
                            stop=(b == R_PASSES - 1 and c == N // P - 1),
                        )
                if piece < SCALAR_PIECES:
                    for c in range(N // P):
                        nc.scalar.activation(result[:, c, :], bank[:, c, :], ACT.Identity, bias=biases[:, c : c + 1])
                else:
                    nc.vector.tensor_tensor(
                        result[:], bank[:], biases[:].unsqueeze(2).to_broadcast([P, N // P, P]), ALU.add
                    )
                first = half * HALF + piece * P
                nc.sync.dma_start(out[:, first : first + P].rearrange("(c p) j -> p c j", p=P), result[:])

        gather_scales()
        gather_words(0)
        quantize_queries(0, 0, round_queries(0, 0))
        gather_words(1)
        gains = keep.tile([P, R_PASSES, PACK], F32, name="gains", tag="stage4", align_bytes=64)
        nc.sync.dma_start(gains[:], gain.rearrange("(b p t) -> p b t", b=R_PASSES, t=PACK))
        for a in range(1, K_PASSES):
            quantize_queries(0, a, round_queries(0, a))
        banks00 = products(0, 0, pass_by_pass)
        banks01 = products(0, 1, [(a, t) for t in range(PACK) for a in reversed(range(K_PASSES))])
        whole = {}
        quantize_queries(1, 0, round_queries(1, 0))
        unit00 = open_unit(0, False, [x[:] for x in banks00], banks00, "00", None)
        weigh(unit00, range(PACK))
        for a in range(1, K_PASSES):
            quantize_queries(1, a, round_queries(1, a))
        unit01 = open_unit(0, True, [x[:] for x in banks01], banks01, "01", "late")
        mix_words, mix_scales, biases = load_mix()
        weigh(unit01, [0, 1])
        rounded00 = interleave(unit00, "rounded")
        weigh(unit01, [2])
        whole[0, 0] = quantize_relevance(unit00, rounded00)
        weigh(unit01, [3])
        banks10 = products(1, 0, bank_by_bank)
        banks11 = products_in_pieces(1, 1)
        unit10 = open_unit(1, False, [x[:] for x in banks10], banks10, "10", "partial10")
        weigh(unit10, range(PACK))
        rounded10 = interleave(unit10, "rounded")
        pieces = [
            open_unit(1, True, [bank[:, t, :] for t in range(PACK)], [bank], "p%d" % n, "partial_p%d" % n)
            for n, bank in enumerate(banks11)
        ]
        whole[1, 0] = quantize_relevance(unit10, rounded10)
        whole[0, 1] = quantize_relevance(unit01, interleave_on_gpsimd(unit01, "rounded01"), "partial10")
        quantized, rounded = [], []
        for n, piece in enumerate(pieces):
            weigh(piece, range(PACK))
            if n < PIECES - 1:
                rounded.append(interleave_on_gpsimd(piece, "rounded" + piece["name"]))
            if n >= 2:
                quantized.append(quantize_relevance(pieces[n - 2], rounded[n - 2]))
        rounded.append(interleave(pieces[-1], "rounded_last"))
        for n in range(PIECES - 2, PIECES):
            quantized.append(quantize_relevance(pieces[n], rounded[n]))
        mix(0)
        mix_in_pieces(1, quantized)
